import numpy as np, ml_dtypes
CORES = [25,29,65,69,153,157,193,197]
N = 8
BF = ml_dtypes.bfloat16
def gentries(a):
    return np.ascontiguousarray(a.reshape(8, 16, -1).transpose(0, 2, 1)).reshape(8, -1)
def gtable(e):
    e = np.asarray(e); return np.ascontiguousarray(e.reshape(8, -1, 16).transpose(0, 2, 1)).reshape(128, -1).astype(np.int32)
U, D, RO, W = 512, 6, 4, 4096
def parts(rng):
    a = (rng.integers(32, 257, (N, 8, 1, U)) * rng.random((N, 8, 16, U))).astype(np.int64)
    s = rng.integers(0, W, (N, 8, D, U))
    w = np.where(rng.random((N, 8, 1, U)) < 0.5, rng.integers(-1, 2, s.shape), rng.integers(-3, 4, s.shape))
    return a, s, w, rng.integers(-300, 501, (N, 8, U))
def pack(a, s, w, b):
    return {"a0": np.ascontiguousarray(a.reshape(N, 128, U)).astype(np.float32).astype(BF), "sr": np.stack([gtable(x.reshape(8, D * U)) for x in s]),
            "wt": np.ascontiguousarray(w.reshape(N, 8, D * U)).astype(np.int32), "bs": np.ascontiguousarray(b).astype(np.int32)}
def setup_inputs(rng):
    return pack(*parts(rng))
def setup_inputs_ties(rng):
    a, s, w, b = parts(rng); a[..., 1::2] = a[..., ::2]
    m = rng.integers(0, 4, (N, 8, 1, U)); pick = rng.integers(0, 2, s.shape); x = s[:, :, :1]; y = s[:, :, 1:2]
    s = np.where(m == 0, x, np.where(m == 1, x ^ pick, np.where(m == 2, np.where(pick == 1, x, y), s)))
    w = np.where(m == 3, -np.abs(w), w); b = np.where(m[:, :, 0] == 3, -np.abs(b) - 1, np.abs(b))
    for v in (s, w, b): v[:, 4:, ..., 1::2] = v[:, 4:, ..., ::2]
    return pack(a, s, w, b)
def setup_inputs_ends(rng):
    a, s, w, b = parts(rng); own = np.arange(N).reshape(N, 1, 1) * U
    s[:, 0] = rng.choice(np.concatenate([np.arange(N) * U, np.arange(N) * U + U - 1]), (N, D, U))
    s[:, 1] = rng.choice(np.array([0, W - 1]), (N, D, U))
    s[:, 2] = own + rng.integers(0, U, (N, D, U))
    s[:, 3] = (own + U + rng.integers(0, W - U, (N, D, U))) & (W - 1)
    s[:, 4] = int(rng.integers(0, N)) * U + rng.integers(0, U, (N, D, U))
    s[:, 4, 0] = s[:, 4, 0] // U * U + np.arange(U)
    s[:, 5] = own + np.arange(U)
    s[:, 6] = np.argsort(rng.random((N, W)), axis=-1)[:, :D * U].reshape(N, D, U)
    return pack(a, s, w, b)
def setup_inputs_full(rng):
    a, s, w, b = parts(rng)
    a[:, 0] = rng.integers(254, 256, (N, 16, U)); a[:, 0] = np.where(rng.random((N, 1, U)) < 0.5, 255, a[:, 0]); a[:, 0, :, 0] = 255
    s[0, 0, :, 0] = 0; w[:, 0] = rng.integers(1, 4, (N, D, U)); b[:, 0] = 1000
    w[:, 1] = -3; b[:, 1] = -1000
    w[:, 2] = 0; b[:, 2] = rng.integers(240, 256, (N, U))
    w[:, 3] = 0; b[:, 3] = rng.choice(np.array([-1, 0, 1, 254, 255, 256]), (N, U))
    a[:, 4] = 255 * rng.integers(0, 2, (N, 16, U)); w[:, 4] = rng.choice(np.array([-3, 3]), (N, D, U)); b[:, 4] = rng.choice(np.array([-1000, 0, 1000]), (N, U))
    o = rng.permutation(16); x = int(rng.integers(200, 255)); h1 = np.zeros(16, np.int64)
    h1[o[0]] = x; h1[o[1]] = x + 1; h1[o[2:]] = 2 * rng.integers(95, 128, 14)
    h2 = h1.copy(); h2[o[0]] = x + 1; h2[o[1]] = x
    a[:, 5] = np.where(rng.integers(0, 2, (N, 1, U)) == 1, h1[:, None], h2[:, None])
    w[:, 5] = np.where(np.arange(D)[:, None] == rng.integers(0, D, (N, 1, U)), 1, 0); b[:, 5] = 0
    a[:, 6:] = rng.integers(0, 4, (N, 2, 16, U)) * (rng.random((N, 2, 16, U)) < 0.3)
    w[:, 6:] = rng.integers(-1, 2, (N, 2, D, U)); b[:, 6:] = rng.integers(-4, 9, (N, 2, U))
    return pack(a, s, w, b)
def setup_inputs_crowd(rng):
    a, s, w, b = parts(rng); a = np.maximum(a, 1); q = int(rng.integers(0, N))
    s = q * U + rng.integers(0, U, s.shape)
    live = [1, 3, 4, 5, 7]
    w[:, live] = rng.integers(1, 4, (N, 5, D, U)); b[:, live] = rng.integers(0, 101, (N, 5, U))
    w[:, 0:3:2] = -rng.integers(0, 4, (N, 2, D, U)); b[:, 0:3:2] = -1000
    u = q * U + np.arange(U); cand = u[(((20 * u) & (W - 1)) // U == q) & ((u & 1) == 1)]
    s[:, 1] = rng.choice(cand, (N, 1, 1)); s[:, 7] = rng.choice(cand, (N, 1, 1))
    for g, t in ((3, 1), (4, 2), (5, D - 1)):
        z = int(rng.integers(0, U)); a[q, g, :, z] = 0
        s[:, g] = q * U + ((z + 1 + rng.integers(0, U - 1, (N, D, U))) & (U - 1)); s[:, g, t] = q * U + z
    return pack(a, s, w, b)
def setup_inputs_spread(rng):
    a, s, w, b = parts(rng)
    a = np.minimum((np.exp2(8 * rng.random((N, 8, 1, U))) * rng.random(a.shape)).astype(np.int64) + 1, 255) * (rng.random((N, 8, 1, U)) > 0.0625)
    s = np.minimum((W * rng.random(s.shape) ** rng.integers(1, 5, (N, 8, 1, 1))).astype(np.int64), W - 1); s[:, 1::2] = W - 1 - s[:, 1::2]
    w = rng.integers(-3, 4, s.shape); b = rng.integers(-1000, 1001, b.shape)
    b[:, ::3] = (np.exp2(9.9 * rng.random((N, 3, U))) * rng.choice(np.array([-1, 1]), (N, 3, U))).astype(np.int64)
    return pack(a, s, w, b)
def check_inputs(d):
    bad = []; x = np.asarray(d["a0"]).astype(np.float32)
    if not np.all((x >= 0) & (x <= 255) & (x == np.floor(x))): bad.append("whole numbers from 0 to 255 in a0")
    for k, lo, hi in (("sr", 0, W - 1), ("wt", -3, 3), ("bs", -1000, 1000)):
        if np.min(d[k]) < lo or np.max(d[k]) > hi: bad.append("range of " + k)
    return bad
def reference(a0, sr, wt, bs):
    a = a0.astype(np.float32).astype(np.int64).reshape(N, 8, 16, U)
    s = np.stack([gentries(x) for x in sr]).astype(np.int64).reshape(N, 8, D, U)
    w = wt.astype(np.int64).reshape(N, 8, 1, D, U); b = bs.astype(np.int64).reshape(N, 8, 1, U)
    for rnd in range(RO):
        every = np.ascontiguousarray(a.transpose(1, 2, 0, 3)).reshape(8, 16, W)
        na, ns = [], []
        for r in range(N):
            p = np.take_along_axis(every, s[r].reshape(8, 1, D * U), 2).reshape(8, 16, D, U)
            v = np.minimum(np.maximum(b[r] + np.add.reduce(w[r] * p, axis=2), 0), 255)
            c = np.add.reduce(p * v[:, :, None, :], axis=1)
            best = np.argmax(c, axis=1)[:, None, :]; worst = np.argmin(c, axis=1)[:, None, :]
            top = np.roll(np.take_along_axis(c, best, 1), -1, axis=0)
            new = (13 * np.take_along_axis(s[r], best, 1) + 7 * np.take_along_axis(s[r], worst, 1) + top) & (W - 1)
            na.append(v); ns.append(np.where(np.arange(D)[None, :, None] == worst, new, s[r]))
        a = np.stack(na); s = np.stack(ns)
    return {"ya": a.reshape(N, 128, U).astype(np.float32).astype(BF), "ys": np.stack([gtable(x.reshape(8, D * U)) for x in s]).astype(np.float32)}

@@ -1,0 +1,563 @@
+from concourse.bass import DstId, RemoteDMATransfer
+from concourse.mybir import AluOpType as ALU, ActivationFunctionType as ACT
+
+N, U, D, RO, W = 8, 512, 6, 4, 4096
+BIG = float(2 ** 26)
+CFG = {"vg": [[(1, 1), (3, 1)], [], [], []], "cyc": 0.00104, "gc": 1.56, "pe": 0.00053, "hop": 0.1, "lag0": 0.06, "ring": 3.0,
+       "la": {"v": 0.03, "s": 0.0, "t": 0.03, "g": 0.0, "y": 0.0},
+       "pri": {"hs": 4.2, "e1s": -3.0, "o0v": -3.1, "e0s": -0.9, "t1v": 3.2, "x0v": -3.1, "v0v": 5.0, "v1v": 0.8, "o0t": -4.4,
+               "e1t": -0.8, "r0v": -8, "ht": 0.7, "g0s": 5.7, "v0t": 4.9, "e0t": 1.8, "v3v": 4.6, "m3v": -0.3, "v2v": -1.3,
+               "o1v": 1.8, "g3v": 7.1, "g2s": 5.0, "g3s": -5.6, "g1s": 2.6, "hv": -1.7, "m2v": 0.1, "v3t": -0.8, "r1v": -4.2,
+               "m1v": 3.6, "m1t": 0.1, "g1v": -1.7, "m0v": -3.8, "t0v": 0.6, "m3t": -0.2, "x1v": -8}}
+
+SCRATCH = {
+    "sa": ("dram", [8, 128, 64], "bfloat16"), "si": ("dram", [8, 128, 48], "int32"), "sb": ("dram", [8, 128, 4], "int32"),
+    "la": ("dram", [8, 128, 64], "bfloat16"), "li": ("dram", [8, 128, 48], "int32"), "lb": ("dram", [8, 128, 4], "int32"),
+    "ra": ("dram", [2, 128, 64], "bfloat16"), "ri": ("dram", [2, 128, 48], "int32"), "rb": ("dram", [2, 128, 4], "int32"),
+    "sy": ("dram", [8, 128, 64], "bfloat16"), "ly": ("dram", [8, 128, 64], "bfloat16"), "ry": ("dram", [2, 128, 64], "bfloat16"),
+    "rk": ("sbuf", [128, 4 * 24], "float32"), "rc": ("sbuf", [128, 6 * 16], "float32"),
+    "mhi": ("sbuf", [128, 128], "float32"), "mlo": ("sbuf", [128, 128], "float32"), "kc": ("sbuf", [128, 4], "int32"),
+    "kf": ("sbuf", [128, 2], "float32"), "blk": ("sbuf", [128, 128], "float32"), "d16": ("sbuf", [128, 128], "float32"),
+    "rm8": ("sbuf", [128, 8], "float32"), "b8": ("sbuf", [128, 8], "float32"),
+    "idh": ("sbuf", [128, 128], "float16"), "idb": ("sbuf", [128, 128], "bfloat16"),
+    "sel": ("sbuf", [128, 2048], "float16"), "rep": ("sbuf", [128, 1024], "bfloat16"), "zz": ("sbuf", [128, 272], "float16"),
+    "dmax": ("sbuf", [128, 96], "float32"), "dmin": ("sbuf", [128, 96], "float32"), "keep": ("sbuf", [128, 96], "float32"),
+    "coff": ("sbuf", [128, 96], "float32"), "coef": ("sbuf", [128, 32], "float32"),
+    "ysr": ("sbuf", [128, 6, 32], "int32"), "wi": ("sbuf", [128, 192], "int32"), "bi": ("sbuf", [128, 256], "int32"),
+    "wf": ("sbuf", [128, 192], "float32"), "bf": ("sbuf", [128, 256], "float32"),
+    "wq": ("sbuf", [128, 192], "float16"), "bq": ("sbuf", [128, 256], "float16"), "py": ("sbuf", [128, 192], "float16"),
+    "win": ("sbuf", [128, 2 * 4096], "bfloat16"), "off": ("sbuf", [128, 192], "uint16"), "vsb": ("sbuf", [128, 512], "bfloat16"),
+    "p": ("sbuf", [128, 3072], "bfloat16"), "pw": ("sbuf", [128, 3072], "float16"), "pv": ("sbuf", [128, 3072], "float32"),
+    "px": ("sbuf", [128, 192], "float16"), "sx": ("sbuf", [128, 192], "float32"),
+    "scb": ("sbuf", [128, 192], "float32"), "scw": ("sbuf", [128, 192], "float32"), "nb": ("sbuf", [128, 192], "float32"),
+    "fpad": ("sbuf", [128, 192], "float32"), "dpad": ("sbuf", [128, 192], "float32"), "bc": ("sbuf", [128, 192], "float32"),
+    "nw": ("sbuf", [128, 192], "float32"), "ew": ("sbuf", [128, 192], "float32"), "s2": ("sbuf", [128, 384], "float32"),
+    "u1": ("sbuf", [128, 64], "float32"), "uu": ("sbuf", [128, 32], "float32"), "tm": ("sbuf", [128, 32], "float32"),
+    "tot": ("sbuf", [128, 32], "int32"), "nwv": ("sbuf", [128, 32], "int32"),
+    "key": ("sbuf", [128, 8 * 16], "float32"), "cin": ("sbuf", [128, 6 * 16], "float32"),
+    "ks": ("sbuf", [128, 192], "float32"), "kl": ("sbuf", [128, 192], "float32"), "sl": ("sbuf", [128, 192], "float32"),
+    "yo": ("sbuf", [128, 6, 32], "float32"),
+    "pw0": ("psum", [128, 512], "float32"), "pw1": ("psum", [128, 512], "float32"),
+    "pe0": ("psum", [128, 512], "float32"), "pe1": ("psum", [128, 512], "float32"),
+    "px0": ("psum", [128, 512], "float32"), "px1": ("psum", [128, 512], "float32"),
+    "pk0": ("psum", [128, 512], "float32"), "pk1": ("psum", [128, 512], "float32"),
+}
+PHASES = ["a", "i", "b", "c0", "c1", "c2", "c3", "c4", "c5", "s0", "s1", "k0", "k1", "y"]
+SEMAPHORES = (["cv", "cs", "ct", "cg", "sent", "dsa", "dsi", "dsb", "doa", "doi", "dob", "dla0", "dla1", "dla2", "dla3", "dls", "dlw", "dlb",
+               "dsy", "doy", "dya", "dys", "ara0", "ara1", "ara2", "ara3"]
+              + ["ar" + p for p in PHASES[1:]] + ["rl" + p for p in PHASES])
+_PLAN = {}
+
+
+def _bits(engines):
+    return sum(1 << e for e in engines)
+
+
+def _perms(xs):
+    if len(xs) <= 1:
+        yield list(xs)
+        return
+    for i in range(len(xs)):
+        for r in _perms(xs[:i] + xs[i + 1:]):
+            yield [xs[i]] + r
+
+
+def make_plan(T, topo):
+    cores = list(T.cores)
+    same = lambda a, b: a in topo.cores_of(b)
+    cost = lambda a, b: 1 if same(a, b) else (3 if topo.may_write(a, b) else 10)
+    best = None
+    for pm in _perms(list(range(1, N))):
+        ring = [0] + pm
+        c = sum(cost(cores[ring[(k + 1) % N]], cores[ring[k]]) for k in range(N))
+        if best is None or c < best[0]:
+            best = (c, ring)
+    ring = best[1]
+    net = [ring.index(r) for r in range(N)]
+    calls, got = {}, {}
+
+    def add(src, ph, transfers):
+        calls.setdefault(src, {}).setdefault(ph, []).append(transfers)
+        for dst, mask, sem, a, b in transfers:
+            got[(dst, sem)] = got.get((dst, sem), 0) + bin(mask).count("1")
+            got[(src, "sent")] = got.get((src, "sent"), 0) + bin(mask).count("1")
+
+    used = set()
+    for r in range(N):
+        c = cores[r]
+        sib = [d for d in range(N) if d != r and same(cores[d], c)]
+        far = [d for d in range(N) if not same(cores[d], c) and topo.may_write(c, cores[d])]
+        oth = [d for d in range(N) if not topo.may_write(c, cores[d]) and d != r]
+        pairs = []
+        for d in oth:
+            if pairs and same(cores[pairs[-1][0]], cores[d]):
+                pairs[-1].append(d)
+            else:
+                pairs.append([d])
+        relay = []
+        for pr in pairs:
+            assert len(pr) == 2 and pr[1] == pr[0] + 1
+            cand = [x for x in topo.cores_of(c) if x not in cores and x not in used and topo.may_write(x, cores[pr[0]])]
+            cand.sort(key=lambda x: topo.die(x) != topo.die(c))
+            relay.append(cand[0])
+            used.add(cand[0])
+        assert len(sib) == 1 and len(far) == 2 and len(pairs) == 2
+        on = topo.engines(c, cores[sib[0]])
+        off = topo.engines(c, cores[far[0]])
+        loc = [e for e in on if e not in off]
+
+        def dram_phase(ph, ar, sname, lname, rname, sslot, lslot, k):
+            tr = []
+            for a in range(2):
+                for b in range(2):
+                    n = 2 * a + b
+                    tr.append((relay[a], _bits(loc[2 * n:2 * n + k]), "rl" + ph, (sname, sslot(pairs[a][b])), (rname, b)))
+            add(c, ph, tr)
+            tr = [(cores[far[b]], _bits(off[2 * b:2 * b + k]), ar, (sname, sslot(far[b])), (lname, lslot)) for b in range(2)]
+            tr.append((cores[sib[0]], _bits(off[4:4 + k]), ar, (sname, sslot(sib[0])), (lname, lslot)))
+            add(c, ph, tr)
+            for a in range(2):
+                ro = topo.engines(relay[a], cores[pairs[a][0]])
+                pick = [ro[0:1], ro[4:5]] if k == 1 else [ro[0:4], ro[4:8]]
+                add(relay[a], ph, [(cores[pairs[a][b]], _bits(pick[b]), ar, (rname, b), (lname, lslot)) for b in range(2)])
+
+        dram_phase("a", "ara%d" % (r // 2), "sa", "la", "ra", lambda d: net[d], r, 1)
+        dram_phase("i", "ari", "si", "li", "ri", lambda d: net[d], r, 2)
+        dram_phase("b", "arb", "sb", "lb", "rb", lambda d: net[d], r, 1)
+        dram_phase("y", "ary", "sy", "ly", "ry", lambda d: d, net[r], 2)
+        for n, (ph, sname, lname) in enumerate([("s0", "sx", "sl"), ("s1", "sx", "sl"), ("k0", "ks", "kl"), ("k1", "ks", "kl")]):
+            o = 96 * (n % 2)
+            land = (lname, o + 12 * net[r], 12)
+            tr = [(relay[a], _bits(on[8 * a:8 * a + 8]), "rl" + ph, (sname, o + 12 * pairs[a][0], 24), ("rk", 24 * n, 24)) for a in range(2)]
+            add(c, ph, tr)
+            tr = [(cores[far[b]], _bits(off[4 * b:4 * b + 4]), "ar" + ph, (sname, o + 12 * far[b], 12), land) for b in range(2)]
+            tr.append((cores[sib[0]], _bits(loc), "ar" + ph, (sname, o + 12 * sib[0], 12), land))
+            add(c, ph, tr)
+            for a in range(2):
+                ro = topo.engines(relay[a], cores[pairs[a][0]])
+                add(relay[a], ph, [(cores[pairs[a][b]], _bits(ro[4 * b:4 * b + 4]), "ar" + ph, ("rk", 24 * n + 12 * b, 12), land) for b in range(2)])
+        d = ring[(net[r] - 1) % N]
+        for n in range(6):
+            ph = "c%d" % n
+            if topo.may_write(c, cores[d]):
+                add(c, ph, [(cores[d], topo.mask(c, cores[d]), "ar" + ph, ("key", 16 * n, 16), ("cin", 16 * n, 16))])
+            else:
+                x = relay[0] if d in pairs[0] else relay[1]
+                add(c, ph, [(x, topo.mask(c, x), "rl" + ph, ("key", 16 * n, 16), ("rc", 16 * n, 16))])
+                add(x, ph, [(cores[d], topo.mask(x, cores[d]), "ar" + ph, ("rc", 16 * n, 16), ("cin", 16 * n, 16))])
+    return {"net": net, "calls": calls, "got": got}
+
+
+def _side(T, s):
+    return T[s[0]][s[1]] if len(s) == 2 else T[s[0]][:, s[1]:s[1] + s[2]]
+
+
+def remote(g, core, T, topo, transfers):
+    tr = []
+    for dst, mask, sem, a, b in transfers:
+        rid, pid = topo.addr(dst, core)
+        tr.append(RemoteDMATransfer(dst_ids=[DstId(rid=rid, pnc=pid)], dma_engine_mask=mask, remote_sem=T.sem[sem],
+                                    src=_side(T, a), dst=_side(T, b)))
+    g.remote_dma_fused(tr, local_sem=T.sem.sent)
+
+
+def arrange(ops):
+    lastw, readers, banks, chain, sent = {}, {}, {}, {}, {}
+    for i, o in enumerate(ops):
+        deps, order = set(), {}
+        for x in o["r"]:
+            deps.update(lastw.get(x, []))
+        for x in o["w"]:
+            deps.update(lastw.get(x, []))
+            deps.update(readers.get(x, []))
+        for b in o["b"]:
+            deps.update(k for e, k in banks.get(b, {}).items() if e != o["e"])
+            if o["e"] in banks.get(b, {}):
+                order[banks[b][o["e"]]] = 0.0
+        if o["e"] in "gy" or o["dma"]:
+            if o["e"] in chain:
+                order[chain[o["e"]]] = 0.0
+            chain[o["e"]] = i
+        deps.discard(i)
+        hard = set()
+        for k in deps:
+            d = ops[k]
+            if (o["e"] == "t" and d["e"] == "t") or (o["dma"] and d["dma"] == o["dma"]) or d["rem"]:
+                order[k] = 0.0
+            else:
+                hard.add(k)
+                d["need"] = True
+                order[k] = 2.2 if d["dma"] else (CFG["lag0"] if d["e"] == o["e"] else CFG["hop"] + (0.1 if d["e"] == "t" else 0.0))
+        if o["after"]:
+            order[sent[o["after"][0]]] = o["after"][1]
+        if o["rem"] and o["rem"] not in sent:
+            sent[o["rem"]] = i
+        o["deps"], o["order"], o["succ"] = hard, order, []
+        for k in order:
+            ops[k]["succ"].append(i)
+        for x in o["r"]:
+            readers.setdefault(x, []).append(i)
+        for x in o["w"]:
+            lastw[x] = [i]
+            readers[x] = []
+        for b in o["b"]:
+            banks.setdefault(b, {})[o["e"]] = i
+    for i in range(len(ops) - 1, -1, -1):
+        o = ops[i]
+        o["level"] = o["c"] + max([ops[k]["level"] + ops[k]["order"][i] for k in o["succ"]] + [0.0])
+        o["left"], o["at"] = len(o["order"]), 0.0
+    ready = {e: [] for e in "vstgy"}
+    free = {e: 0.0 for e in "vstgy"}
+    for i, o in enumerate(ops):
+        if o["left"] == 0:
+            ready[o["e"]].append(i)
+    out = []
+    while len(out) < len(ops):
+        e = min((x for x in ready if ready[x]), key=lambda x: max(free[x], min(ops[k]["at"] for k in ready[x])))
+        now = max(free[e], min(ops[k]["at"] for k in ready[e]))
+        i = max((k for k in ready[e] if ops[k]["at"] <= now + CFG["la"][e]),
+                key=lambda k: (ops[k]["level"] + CFG["pri"].get(ops[k]["tag"] + e, 0.0), -k))
+        ready[e].remove(i)
+        o = ops[i]
+        free[e] = max(now, o["at"]) + o["c"]
+        out.append(i)
+        for k in o["succ"]:
+            s = ops[k]
+            s["at"] = max(s["at"], free[e] + s["order"][i])
+            s["left"] -= 1
+            if s["left"] == 0:
+                ready[s["e"]].append(k)
+    return out
+
+
+def emit(g, T, ops):
+    queue = {"v": g.vector, "s": g.scalar, "t": g.tensor, "g": g, "y": g.sync}
+    counter = {"v": "cv", "s": "cs", "t": "ct", "g": "cg"}
+    ndma, count, known = {}, {}, {}
+    for o in ops:
+        if o["dma"]:
+            ndma[o["dma"]] = ndma.get(o["dma"], 0) + 1
+    for i in arrange(ops):
+        o = ops[i]
+        q = queue[o["e"]]
+        want = {}
+        for k in o["deps"]:
+            d = ops[k]
+            s, val = (d["dma"], 16 * ndma[d["dma"]]) if d["dma"] else (counter[d["e"]], d["n"])
+            want[s] = max(want.get(s, 0), val)
+        for s, val in o["wait"]:
+            want[s] = max(want.get(s, 0), val)
+        for s, val in want.items():
+            if known.get((o["e"], s), 0) < val:
+                q.wait_ge(T.sem[s], val)
+                known[(o["e"], s)] = val
+        ins = o["f"](q)
+        if o["dma"]:
+            ins.then_inc(T.sem[o["dma"]], 16)
+        elif o.get("need"):
+            count[o["e"]] = count.get(o["e"], 0) + 1
+            o["n"] = count[o["e"]]
+            ins.then_inc(T.sem[counter[o["e"]]], 1)
+    for e, n in count.items():
+        g.wait_ge(T.sem[counter[e]], n)
+    for s, n in ndma.items():
+        g.sync.wait_ge(T.sem[s], 16 * n)
+
+
+def rank_program(g, core, T, topo):
+    if "p" not in _PLAN:
+        _PLAN["p"] = make_plan(T, topo)
+    plan = _PLAN["p"]
+    calls, got = plan["calls"].get(core), plan["got"]
+    rank = T.rank_of(core)
+    if calls is None:
+        return
+    if rank is None:
+        for ph in PHASES:
+            if ph in calls:
+                g.wait_ge(T.sem["rl" + ph], got[(core, "rl" + ph)])
+                for tr in calls[ph]:
+                    remote(g, core, T, topo, tr)
+        g.wait_ge(T.sem.sent, got[(core, "sent")])
+        return
+    me = plan["net"][rank]
+    cores = list(T.cores)
+    ops = []
+    tag = ["h"]
+    cyc, pe = CFG["cyc"], CFG["pe"]
+
+    def op(e, f, c, r=(), w=(), b=(), arr=None, dma=None, rem=None):
+        wait = [(arr[0], got[(core, arr[0])])] if arr else []
+        ops.append({"e": e, "f": f, "c": c, "r": list(r), "w": list(w), "b": list(b), "wait": wait,
+                    "after": arr[1:] if arr else None, "dma": dma, "rem": rem, "tag": tag[0]})
+
+    def send(ph, reads):
+        for tr in calls[ph]:
+            op("g", lambda q, tr=tr: remote(g, core, T, topo, tr), 0.3, r=reads, rem=ph)
+
+    def dma(e, sem, out, in_, r=(), w=(), arr=None):
+        op(e, lambda q: q.dma_start(out, in_), 0.05, r=r, w=w, arr=arr, dma=sem)
+
+    def ts(n, out, in0, s1, s2, o0, o1, r, w, b=()):
+        if o1 is None:
+            op("v", lambda q: q.tensor_scalar(out, in0, s1, None, o0), n * cyc, r, w, b)
+        else:
+            op("v", lambda q: q.tensor_scalar(out, in0, s1, s2, o0, o1), n * cyc, r, w, b)
+
+    def tt(n, out, in0, in1, o, r, w, b=(), arr=None):
+        op("v", lambda q: q.tensor_tensor(out, in0, in1, o), n * cyc, r, w, b, arr)
+
+    def cp(n, out, in_, r, w, b=(), arr=None):
+        op("v", lambda q: q.tensor_copy(out, in_), n * cyc, r, w, b, arr)
+
+    def scan(out, d0, d1, o0, o1, r, w, b=()):
+        op("v", lambda q: q.tensor_tensor_scan(out, d0, d1, 0.0, o0, o1), 96 * cyc, r, w, b)
+
+    def fill(n, ap, val, w):
+        op("v", lambda q: q.memset(ap, val), n * cyc, (), w)
+
+    def mm(n, out, lhsT, rhs, start, stop, r, w, b):
+        op("t", lambda q: q.matmul(out, lhsT, rhs, start, stop), n * pe, r, w, b)
+
+    def act(n, out, in_, r, w, b=()):
+        op("s", lambda q: q.activation(out, in_, ACT.Copy), n * cyc, r, w, b)
+
+    PW, PE, PX, PK = [T.pw0, T.pw1], [T.pe0, T.pe1], [T.px0, T.px1], [T.pk0, T.pk1]
+
+    dma("y", "dsa", T.sa[:], T.a0[:], w=["sa"])
+    dma("s", "dsi", T.si[:, 0:64, :], T.sr[:], w=["si0"])
+    dma("s", "dsi", T.si[:, 64:128, :], T.wt[:], w=["si1"])
+    dma("s", "dsb", T.sb[:], T.bs[:], w=["sb"])
+    dma("y", "doa", T.la[rank], T.a0[16 * me:16 * me + 16, :], w=["la"])
+    dma("y", "doi", T.li[rank, 0:64, :], T.sr[16 * me:16 * me + 16, :], w=["li0"])
+    dma("y", "doi", T.li[rank, 64:128, :], T.wt[me:me + 1, :], w=["li1"])
+    dma("y", "dob", T.lb[rank], T.bs[me:me + 1, :], w=["lb"])
+    op("g", lambda q: q.iota(T.kc[:, 0:1], [[0, 1]], 0, 1), 0.14, w=["kc0"])
+    op("g", lambda q: q.iota(T.mlo[:], [[0, 8], [1, 16]], 0, 0, allow_small_or_imprecise_dtypes=True), 0.4, w=["mlo"])
+    op("g", lambda q: q.iota(T.mhi[:], [[1, 8], [0, 16]], 0, 0, allow_small_or_imprecise_dtypes=True), 0.4, w=["mhi"])
+    send("a", ["sa"])
+    send("i", ["si0", "si1"])
+    send("b", ["sb"])
+    blocks = sorted(range(4), key=lambda k: (k != rank // 2, not topo.may_write(cores[2 * k], core)))
+    for n, k in enumerate(blocks):
+        dma("y", "dla%d" % k, T.vsb[32 * k:32 * k + 32, :], T.la[2 * k:2 * k + 2], r=["la"], w=["va%d" % k],
+            arr=("ara%d" % k, "a", 4.5 if n < 2 else 8.0))
+    dma("y", "dls", T.ysr[:], T.li[:, 0:64, :], r=["li0"], w=["ysr"], arr=("ari", "i", 6.5))
+    dma("y", "dlw", T.wi[:], T.li[:, 64:128, :], r=["li1"], w=["wi"])
+    fill(256, T.bi[:], 0, ["bi0", "bi1"])
+    for h in range(2):
+        dma("y", "dlb", T.bi[h::16, :], T.lb[:, 64 * h:64 * h + 64, :], r=["lb"], w=["bi%d" % h], arr=("arb", "b", 6.0))
+    fill(96, T.dmax[:], 1.0, ["dmax"])
+    fill(96, T.dmin[:], -1.0, ["dmin"])
+    fill(96, T.keep[:], 1.0, ["keep"])
+    fill(192, T.fpad[:], -1.0, ["fpad0", "fpad1"])
+    fill(192, T.dpad[:], -4096.0, ["dpad0", "dpad1"])
+    fill(64, T.coef[:, 0:16], 104.0, ["coefa"])
+    fill(64, T.coef[:, 16:32], 56.0, ["coefb"])
+    fill(192, T.bc[:], 0.0, ["bc0", "bc1"])
+    for s in range(D):
+        fill(64, T.coff[:, s::6], float(4096 * (5 - s) + 2048), ["coff%d" % s])
+    coff = ["coff%d" % s for s in range(D)]
+    fill(64, T.dmax[:, 0::6], -BIG, ["dmax"])
+    fill(64, T.dmin[:, 0::6], BIG, ["dmin"])
+    fill(64, T.keep[:, 0::6], 0.0, ["keep"])
+    cp(192, T.zz[:, 0:192], T.bc[:, 0:192], ["bc0", "bc1"], ["zza"])
+    cp(80, T.zz[:, 192:272], T.bc[:, 0:80], ["bc0", "bc1"], ["zzb"])
+    ts(64, T.kc[:, 1:2], T.kc[:, 0:1], 4, None, ALU.arith_shift_right, None, ["kc0"], ["kc1"])
+    ts(64, T.kc[:, 2:3], T.kc[:, 0:1], 15, None, ALU.bitwise_and, None, ["kc0"], ["kc2"])
+    cp(64, T.kf[:], T.kc[:, 1:3], ["kc1", "kc2"], ["kf"])
+    ts(128, T.d16[:], T.mlo[:], T.kf[:, 1:2], None, ALU.is_equal, None, ["mlo", "kf"], ["d16"])
+    ts(64, T.rm8[:], T.mlo[:, 0:8], T.kf[:, 0:1], None, ALU.is_equal, None, ["mlo", "kf"], ["rm8"])
+    ts(128, T.blk[:], T.mhi[:], T.kf[:, 0:1], None, ALU.is_equal, None, ["mhi", "kf"], ["blk"])
+    for j in range(8):
+        ts(128, T.rep[:, 128 * j:128 * j + 128], T.d16[:], T.rm8[:, j:j + 1], None, ALU.mult, None, ["d16", "rm8"], ["rep%d" % j])
+    for j in range(8):
+        ts(64, T.zz[:, 16 + 32 * j:32 + 32 * j], T.d16[:, 0:16], T.rm8[:, j:j + 1], None, ALU.mult, None, ["d16", "rm8", "zza", "zzb"], ["zz%d" % j])
+    tt(256, T.idh[:], T.d16[:], T.blk[:], ALU.mult, ["d16", "blk"], ["idh"])
+    tt(256, T.idb[:], T.d16[:], T.blk[:], ALU.mult, ["d16", "blk"], ["idb"])
+    ts(64, T.b8[:], T.rm8[:], 8.0, None, ALU.mult, None, ["rm8"], ["b8"])
+    for c in range(16):
+        ts(128, T.sel[:, 128 * c:128 * c + 128], T.blk[:], T.d16[:, c:c + 1], None, ALU.mult, None, ["d16", "blk"], ["sel%d" % c])
+
+    winall = lambda u: ["win%d_%d_%d" % (u, j, h) for j in range(8) for h in range(2)]
+    vall = ["v0", "v1", "v2", "v3"]
+
+    rot = [(T.pe0, "pe0"), (T.pe1, "pe1"), (T.px0, "px0"), (T.px1, "px1"), (T.pk0, "pk0"), (T.pk1, "pk1"), (T.pw0, "pw0"), (T.pw1, "pw1")]
+    for n, j in enumerate([2 * k + i for k in blocks for i in range(2)]):
+        k = j // 2
+        ps, bank = rot[n]
+        mm(512, ps[:], T.rep[32 * k:32 * k + 32, 128 * j:128 * j + 128], T.vsb[32 * k:32 * k + 32, :], True, True,
+           ["rep%d" % j, "va%d" % k], ["first%d" % j], [bank])
+        (act if n % 2 else cp)(512, T.win[:, 512 * j:512 * j + 512], ps[:], ["first%d" % j], ["win0_%d_0" % j, "win0_%d_1" % j], [bank])
+    for qq in range(4):
+        cp(64, T.off[:, 48 * qq:48 * qq + 48], T.ysr[:, :, 8 * qq:8 * qq + 8], ["ysr"], ["off%d" % qq])
+    cp(192, T.wf[:], T.wi[:], ["wi"], ["wf"])
+    cp(256, T.bf[:], T.bi[:], ["bi0", "bi1"], ["bf"])
+    cp(192, T.wq[:], T.wf[:], ["wf"], ["wq"])
+    cp(256, T.bq[:], T.bf[:], ["bf"], ["bq"])
+
+    def place(out, a, rhs, r, w, b):
+        mm(32, out(32), T.zz[:, 32 * a:32 * a + 32], rhs(1), True, False, r + ["zz%d" % a], w, b)
+        mm(16, out(16), T.zz[:, 32 * a + 16:32 * a + 32], rhs(0), False, True, r + ["zz%d" % a], w, b)
+
+    def first_sources(h):
+        a = 96 * h
+        cp(96, T.bc[:, a:a + 96], T.off[:, a:a + 96], ["off%d" % (2 * h), "off%d" % (2 * h + 1)], ["bc%d" % h])
+        ts(96, T.py[:, a:a + 96], T.bc[:, a:a + 96], -2048.0, None, ALU.add, None, ["bc%d" % h], ["py%d" % h])
+        for j in range(8):
+            for n in range(4):
+                place(lambda m: PK[h][32 * n:32 * n + m, 128 + 12 * j:140 + 12 * j], j,
+                      lambda lo: T.py[:, a + 2 * n + lo:a + 96:8], ["py%d" % h], ["cv%d" % h], ["pk%d" % h])
+        cp(96, T.px[:, a:a + 96], PK[h][:, 128:224], ["cv%d" % h], ["px%d" % h], ["pk%d" % h])
+        tt(96, T.sx[:, a:a + 96], PK[h][:, 128:224], T.coff[:], ALU.add, ["cv%d" % h] + coff, ["sx%d" % h], ["pk%d" % h])
+
+    def gather(q, k, eng, u):
+        tag[0] = "g%d" % q
+        c = 768 * q + 384 * k
+        src = lambda: T.win[:, W * u:W * u + W].indirect(T.off[:, 48 * q + 24 * k:48 * q + 24 * k + 24])
+        r, w, cost = winall(u) + ["off%d" % q], ["p%d_%d" % (q, k)], 0.06 + 384 * CFG["gc"] * cyc
+        if eng == "s":
+            op("s", lambda e: e.activation(T.p[:, c:c + 384], src(), ACT.Copy), cost, r, w)
+        else:
+            op("v", lambda e: e.tensor_copy(T.p[:, c:c + 384], src()), cost, r, w)
+
+    def sums(q, k):
+        h, b = q // 2, q % 2
+        tag[0] = "m%d" % q
+        for s in range(3 * k, 3 * k + 3):
+            e0 = 512 * s + 128 * q
+            e = e0
+            while e < e0 + 128:
+                c = e // 192
+                n = min(e0 + 128, 192 * (c + 1)) - e
+                o = 128 * (s - 3 * k) + e - e0
+                mm(n, PW[k][:, o:o + n], T.sel[:, 128 * c:128 * c + 128], T.wq[:, e - 192 * c:e - 192 * c + n], True, True,
+                   ["wq", "sel%d" % c], ["pw%d" % k], ["pw%d" % k])
+                e += n
+        c = 768 * q + 384 * k
+        tt(384, T.pw[:, c:c + 384], T.p[:, c:c + 384], PW[k][:, 0:384], ALU.mult, ["p%d_%d" % (q, k), "pw%d" % k], ["m%d_%d" % (q, k)], ["pw%d" % k])
+        out = PX[b][:, 0:128]
+        if k == 0:
+            mm(128, out, T.sel[:, 128 * h:128 * h + 128], T.bq[:, 128 * b:128 * b + 128], True, False, ["bq", "sel%d" % h], ["x%d" % b], ["px%d" % b])
+        for s in range(3 * k, 3 * k + 3):
+            c = 768 * q + 128 * s
+            mm(128, out, T.idh[:], T.pw[:, c:c + 128], False, s == 5, ["idh", "m%d_%d" % (q, k)], ["x%d" % b], ["px%d" % b])
+
+    def clamp(q):
+        b, c = q % 2, 128 * q
+        ts(128, T.vsb[:, c:c + 128], PX[b][:, 0:128], 0.0, 255.0, ALU.max, ALU.min, ["x%d" % b], ["v%d" % q, "va0", "va1", "va2", "va3"], ["px%d" % b])
+        mm(128, PX[b][:, 0:128], T.idb[:], T.vsb[:, c:c + 128], True, True, ["idb", "v%d" % q], ["x%d" % b], ["px%d" % b])
+
+    def spread(h, u):
+        tag[0] = "e%d" % h
+        for jj in range(4):
+            bank = ["pe%d" % (jj % 2)]
+            for j in (2 * jj, 2 * jj + 1):
+                mm(256, PE[jj % 2][:, 256 * (j % 2):256 * (j % 2) + 256], T.rep[:, 128 * j:128 * j + 128], T.vsb[:, 256 * h:256 * h + 256],
+                   True, True, ["v%d" % (2 * h), "v%d" % (2 * h + 1), "rep%d" % j], bank, bank)
+            for j in (2 * jj, 2 * jj + 1):
+                act(256, T.win[:, W * u + 512 * j + 256 * h:W * u + 512 * j + 256 * h + 256], PE[jj % 2][:, 256 * (j % 2):256 * (j % 2) + 256],
+                    bank, ["win%d_%d_%d" % (u, j, h)], bank)
+
+    def scores(q):
+        h, b = q // 2, q % 2
+        tag[0] = "v%d" % q
+        for s in range(D):
+            c = 768 * q + 128 * s
+            tt(128, T.pv[:, c:c + 128], T.p[:, c:c + 128], PX[b][:, 0:128], ALU.mult,
+               ["p%d_%d" % (q, s // 3), "x%d" % b], ["pv%d_%d" % (q, s)], ["px%d" % b])
+            mm(256, PK[h][:, 6 * b + s:96:12], T.pv[:, c:c + 128], T.b8[:], True, True, ["pv%d_%d" % (q, s), "b8"], ["k%d" % h], ["pk%d" % h])
+
+    def renew(h, slot, own):
+        H = str(h)
+        tag[0] = "t" + H
+        a, z = 96 * h, 16 * h
+        K, kb = PK[h][:, 0:96], ["pk" + H]
+        c96 = lambda t: t[:, a:a + 96]
+        c16 = lambda t: t[:, z:z + 16]
+        last = lambda t: t[:, a + 5:a + 96:6]
+        sx, sxn, keyn = (T.sl if own else T.sx), ("sl" if own else "sx") + H, "key%d" % slot
+        scan(c96(T.scb), T.dmax[:], K, ALU.add, ALU.max, ["dmax", "k" + H], ["scb" + H], kb)
+        scan(c96(T.scw), T.dmin[:], K, ALU.add, ALU.min, ["dmin", "k" + H], ["scw" + H], kb)
+        cp(64, T.key[:, 16 * slot:16 * slot + 16], last(T.scb), ["scb" + H], [keyn])
+        if not own:
+            send("c%d" % slot, [keyn])
+        tag[0] = "r" + H
+        ts(64, T.fpad[:, a:a + 96:6], last(T.scw), 5.0, None, ALU.add, None, ["scw" + H], ["fpad" + H])
+        tt(96, c96(T.nb), c96(T.scb), K, ALU.not_equal, ["scb" + H, "k" + H], ["nb" + H], kb)
+        scan(c96(T.bc), T.keep[:], c96(T.fpad), ALU.mult, ALU.add, ["keep", "fpad" + H], ["bc" + H])
+        scan(T.s2[:, 2 * a:2 * a + 96], c96(T.nb), c96(sx), ALU.mult, ALU.max, ["nb" + H, sxn], ["s2b" + H])
+        tt(96, c96(T.nw), c96(T.bc), K, ALU.not_equal, ["bc" + H, "k" + H], ["nw" + H], kb)
+        tt(96, c96(T.ew), c96(T.bc), K, ALU.is_equal, ["bc" + H, "k" + H], ["ew" + H], kb)
+        scan(T.s2[:, 2 * a + 96:2 * a + 192], c96(T.nw), c96(sx), ALU.mult, ALU.max, ["nw" + H, sxn], ["s2w" + H])
+        tt(64, T.u1[:, 2 * z:2 * z + 32], T.s2[:, 2 * a + 5:2 * a + 192:6], T.coef[:], ALU.mult, ["s2b" + H, "s2w" + H, "coefa", "coefb"], ["u1" + H])
+        tt(64, c16(T.uu), T.u1[:, 2 * z:2 * z + 16], T.u1[:, 2 * z + 16:2 * z + 32], ALU.add, ["u1" + H], ["uu" + H])
+        ts(64, c16(T.tm), T.s2[:, 2 * a + 101:2 * a + 192:6], -20480.0, None, ALU.add, None, ["s2w" + H], ["tm" + H])
+        tag[0] = "o" + H
+        if own:
+            tt(64, T.tot[:, z:z + 14], T.uu[:, z:z + 14], T.key[:, 16 * slot + 2:16 * slot + 16], ALU.add, ["uu" + H, keyn], ["tot" + H])
+            tt(64, T.tot[:, z + 14:z + 16], T.uu[:, z + 14:z + 16], T.key[:, 16 * slot:16 * slot + 2], ALU.add, ["uu" + H, keyn], ["totb" + H])
+        else:
+            tt(64, c16(T.tot), c16(T.uu), T.cin[:, 16 * slot:16 * slot + 16], ALU.add, ["uu" + H], ["tot" + H, "totb" + H],
+               arr=("arc%d" % slot, "c%d" % slot, CFG["ring"]))
+        db, ed = PK[h][:, 256:352], PK[h][:, 384:480]
+        ts(64, c16(T.nwv), c16(T.tot), 3, 4095, ALU.arith_shift_right, ALU.bitwise_and, ["tot" + H, "totb" + H], ["nwv" + H])
+        tt(64, T.dpad[:, a:a + 96:6], c16(T.nwv), c16(T.tm), ALU.subtract, ["nwv" + H, "tm" + H], ["dpad" + H])
+        scan(db, T.keep[:], c96(T.dpad), ALU.mult, ALU.add, ["keep", "dpad" + H], ["db" + H], kb)
+        tt(96, ed, c96(T.ew), db, ALU.mult, ["ew" + H, "db" + H], ["ed" + H], kb)
+        tt(96, c96(T.px), c96(T.px), ed, ALU.add, ["px" + H, "ed" + H], ["px" + H], kb)
+        for n in range(8):
+            for jj in range(4):
+                place(lambda m: PK[h][32 * jj:32 * jj + m, 128 + n:224:8], n,
+                      lambda lo: T.px[:, a + 12 * (2 * jj + lo):a + 12 * (2 * jj + lo) + 12], ["px" + H], ["cv" + H], kb)
+        if own:
+            for b in range(2):
+                ts(64, T.yo[:, :, 16 * h + 8 * b:16 * h + 8 * b + 8], PK[h][:, 128 + 48 * b:176 + 48 * b], 2048.0, None, ALU.add, None,
+                   ["cv" + H], ["yo%d" % (2 * h + b)], kb)
+        else:
+            ts(96, c96(T.off), PK[h][:, 128:224], 2048.0, None, ALU.add, None, ["cv" + H], ["off%d" % (2 * h), "off%d" % (2 * h + 1)], kb)
+            tag[0] = "x" + H
+            tt(96, c96(T.sx), c96(T.sx), ed, ALU.add, ["sx" + H, "ed" + H], ["sx" + H], kb)
+
+    first_sources(0)
+    first_sources(1)
+    for t in range(RO):
+        for q in range(4):
+            for k in range(2):
+                gather(q, k, "v" if (q, k) in CFG["vg"][t] else "s", t % 2)
+        for q in range(4):
+            if q >= 2:
+                scores(q - 2)
+            sums(q, 0)
+            sums(q, 1)
+            clamp(q)
+        scores(2)
+        scores(3)
+        if t < RO - 1:
+            spread(0, (t + 1) % 2)
+            spread(1, (t + 1) % 2)
+            for h in range(2):
+                renew(h, 2 * t + h, False)
+            if t == RO - 2:
+                send("s0", ["sx0"])
+                send("s1", ["sx1"])
+    dma("y", "dsy", T.sy[:], T.vsb[:], r=vall, w=["sy"])
+    dma("y", "doy", T.ly[me], T.vsb[16 * rank:16 * rank + 16, :], r=vall, w=["ly"])
+    for h in range(2):
+        a = 96 * h
+        tag[0] = "t%d" % h
+        cp(96, T.ks[:, a:a + 96], PK[h][:, 0:96], ["k%d" % h], ["ks%d" % h], ["pk%d" % h])
+        send("k%d" % h, ["ks%d" % h])
+        cp(64, T.kl[:, a + 12 * me:a + 12 * me + 12], T.ks[:, a + 12 * rank:a + 12 * rank + 12], ["ks%d" % h], ["kl%d" % h])
+        cp(64, T.sl[:, a + 12 * me:a + 12 * me + 12], T.sx[:, a + 12 * rank:a + 12 * rank + 12], ["sx%d" % h], ["slo%d" % h])
+    send("y", ["sy"])
+    dma("y", "dya", T.ya[:], T.ly[:], r=["ly"], arr=("ary", "y", 5.0))
+    for h in range(2):
+        a = 96 * h
+        tt(192, T.px[:, a:a + 96], T.sl[:, a:a + 96], T.coff[:], ALU.subtract, ["slo%d" % h] + coff, ["px%d" % h, "sl%d" % h],
+           arr=("ars%d" % h, "s%d" % h, 6.5))
+        cp(96, PK[h][:, 0:96], T.kl[:, a:a + 96], ["kl%d" % h], ["k%d" % h], ["pk%d" % h], arr=("ark%d" % h, "k%d" % h, 6.0))
+        renew(h, 6 + h, True)
+    dma("s", "dys", T.ys[:], T.yo[:], r=["yo0", "yo1", "yo2", "yo3"])
+    emit(g, T, ops)
+    g.wait_ge(T.sem.sent, got[(core, "sent")])

@@ -3,50 +3,54 @@ from concourse.mybir import AluOpType as ALU, ActivationFunctionType as ACT
 
 N, U, D, RO, W = 8, 512, 6, 4, 4096
 BIG = float(2 ** 26)
-CFG = {"vg": [[(1, 1), (3, 1)], [], [], []], "cyc": 0.00104, "gc": 1.56, "pe": 0.00053, "hop": 0.1, "lag0": 0.06, "ring": 3.0,
-       "la": {"v": 0.03, "s": 0.0, "t": 0.03, "g": 0.0, "y": 0.0},
-       "pri": {"hs": 4.2, "e1s": -3.0, "o0v": -3.1, "e0s": -0.9, "t1v": 3.2, "x0v": -3.1, "v0v": 5.0, "v1v": 0.8, "o0t": -4.4,
-               "e1t": -0.8, "r0v": -8, "ht": 0.7, "g0s": 5.7, "v0t": 4.9, "e0t": 1.8, "v3v": 4.6, "m3v": -0.3, "v2v": -1.3,
-               "o1v": 1.8, "g3v": 7.1, "g2s": 5.0, "g3s": -5.6, "g1s": 2.6, "hv": -1.7, "m2v": 0.1, "v3t": -0.8, "r1v": -4.2,
-               "m1v": 3.6, "m1t": 0.1, "g1v": -1.7, "m0v": -3.8, "t0v": 0.6, "m3t": -0.2, "x1v": -8}}
+CFG = {"cyc": 0.00086, "gc": 1.56, "pe": 0.00046, "hop": 0.2, "lag0": 0.05, "ring": 2.2, "second": {}, "least": 0.1, "vspread": [], "vfirst": [0, 2, 4, 6],
+       "ta": [3.0, 5.6], "tw": 5.6, "tp": 5.0, "tk": 4.0, "nd": 8, "td": [3.0, 3.6], "early": 3, "uuv": 0, "twice": [], "xbank": [0, 1, 0, 1],
+       "aclamp": [], "fine": 0, "fused": [0, 4], "tries": 3000,
+       "tails": {"k2": 11.0, "k3": 9.5, "y1": 7.0}}
 
 SCRATCH = {
-    "sa": ("dram", [8, 128, 64], "bfloat16"), "si": ("dram", [8, 128, 48], "int32"), "sb": ("dram", [8, 128, 4], "int32"),
-    "la": ("dram", [8, 128, 64], "bfloat16"), "li": ("dram", [8, 128, 48], "int32"), "lb": ("dram", [8, 128, 4], "int32"),
-    "ra": ("dram", [2, 128, 64], "bfloat16"), "ri": ("dram", [2, 128, 48], "int32"), "rb": ("dram", [2, 128, 4], "int32"),
-    "sy": ("dram", [8, 128, 64], "bfloat16"), "ly": ("dram", [8, 128, 64], "bfloat16"), "ry": ("dram", [2, 128, 64], "bfloat16"),
-    "rk": ("sbuf", [128, 4 * 24], "float32"), "rc": ("sbuf", [128, 6 * 16], "float32"),
-    "mhi": ("sbuf", [128, 128], "float32"), "mlo": ("sbuf", [128, 128], "float32"), "kc": ("sbuf", [128, 4], "int32"),
-    "kf": ("sbuf", [128, 2], "float32"), "blk": ("sbuf", [128, 128], "float32"), "d16": ("sbuf", [128, 128], "float32"),
-    "rm8": ("sbuf", [128, 8], "float32"), "b8": ("sbuf", [128, 8], "float32"),
-    "idh": ("sbuf", [128, 128], "float16"), "idb": ("sbuf", [128, 128], "bfloat16"),
-    "sel": ("sbuf", [128, 2048], "float16"), "rep": ("sbuf", [128, 1024], "bfloat16"), "zz": ("sbuf", [128, 272], "float16"),
-    "dmax": ("sbuf", [128, 96], "float32"), "dmin": ("sbuf", [128, 96], "float32"), "keep": ("sbuf", [128, 96], "float32"),
-    "coff": ("sbuf", [128, 96], "float32"), "coef": ("sbuf", [128, 32], "float32"),
-    "ysr": ("sbuf", [128, 6, 32], "int32"), "wi": ("sbuf", [128, 192], "int32"), "bi": ("sbuf", [128, 256], "int32"),
-    "wf": ("sbuf", [128, 192], "float32"), "bf": ("sbuf", [128, 256], "float32"),
-    "wq": ("sbuf", [128, 192], "float16"), "bq": ("sbuf", [128, 256], "float16"), "py": ("sbuf", [128, 192], "float16"),
+    "sa": ("dram", [8, 128, 64], "bfloat16"), "sw": ("dram", [8, 128, 28], "int32"), "sy": ("dram", [8, 128, 64], "bfloat16"),
+    "lw": ("dram", [8, 128, 28], "int32"), "ly": ("dram", [8, 128, 64], "bfloat16"),
+    "ra": ("dram", [2, 128, 64], "bfloat16"), "rw": ("dram", [2, 128, 28], "int32"), "ry": ("dram", [2, 128, 64], "bfloat16"),
+    "rk": ("sbuf", [128, 4 * 12], "float32"), "rc": ("sbuf", [128, 6 * 16], "float32"),
+    "rp": ("sbuf", [128, 48], "float16"), "rs": ("sbuf", [128, 48], "float16"),
+    "ja": ("sbuf", [128, 128], "bfloat16"), "jb": ("sbuf", [128, 8], "bfloat16"), "jd": ("sbuf", [128, 128], "bfloat16"),
+    "jw": ("sbuf", [128, 128], "bfloat16"), "jv": ("sbuf", [128, 128], "bfloat16"), "jp": ("sbuf", [128, 128], "bfloat16"),
+    "jq": ("sbuf", [128, 128], "bfloat16"), "jr": ("sbuf", [128, 128], "bfloat16"),
+    "top": ("sbuf", [128, 1], "float32"), "b8": ("sbuf", [128, 24], "float32"), "jz": ("sbuf", [128, 256], "bfloat16"),
+    "idf": ("sbuf", [128, 128], "float32"), "idh": ("sbuf", [128, 128], "float16"), "idb": ("sbuf", [128, 128], "bfloat16"),
+    "i104": ("sbuf", [128, 128], "float16"), "i56": ("sbuf", [128, 128], "float16"),
+    "turn": ("sbuf", [128, 128], "float16"), "unturn": ("sbuf", [128, 128], "bfloat16"),
+    "sel": ("sbuf", [128, 15 * 128], "float16"), "rep": ("sbuf", [128, 16 * 128], "bfloat16"), "zz": ("sbuf", [128, 256], "float16"),
+    "dmax": ("sbuf", [128, 96], "float32"), "dmin": ("sbuf", [128, 96], "float32"), "drev": ("sbuf", [128, 96], "float32"),
+    "keep": ("sbuf", [128, 96], "float32"), "keeph": ("sbuf", [128, 96], "float16"),
+    "coff": ("sbuf", [128, 112], "float32"), "coffh": ("sbuf", [128, 112], "float16"),
+    "ysr": ("sbuf", [128, 6, 32], "int32"), "py": ("sbuf", [128, 192], "float16"), "pq": ("sbuf", [128, 192], "float16"),
+    "wi": ("sbuf", [128, 256], "int32"), "wq": ("sbuf", [128, 256], "float16"), "va": ("sbuf", [128, 512], "bfloat16"),
     "win": ("sbuf", [128, 2 * 4096], "bfloat16"), "off": ("sbuf", [128, 192], "uint16"), "vsb": ("sbuf", [128, 512], "bfloat16"),
     "p": ("sbuf", [128, 3072], "bfloat16"), "pw": ("sbuf", [128, 3072], "float16"), "pv": ("sbuf", [128, 3072], "float32"),
-    "px": ("sbuf", [128, 192], "float16"), "sx": ("sbuf", [128, 192], "float32"),
+    "px": ("sbuf", [128, 192], "float16"), "wk": ("sbuf", [128, 1536], "bfloat16"),
     "scb": ("sbuf", [128, 192], "float32"), "scw": ("sbuf", [128, 192], "float32"), "nb": ("sbuf", [128, 192], "float32"),
-    "fpad": ("sbuf", [128, 192], "float32"), "dpad": ("sbuf", [128, 192], "float32"), "bc": ("sbuf", [128, 192], "float32"),
-    "nw": ("sbuf", [128, 192], "float32"), "ew": ("sbuf", [128, 192], "float32"), "s2": ("sbuf", [128, 384], "float32"),
-    "u1": ("sbuf", [128, 64], "float32"), "uu": ("sbuf", [128, 32], "float32"), "tm": ("sbuf", [128, 32], "float32"),
-    "tot": ("sbuf", [128, 32], "int32"), "nwv": ("sbuf", [128, 32], "int32"),
+    "bc": ("sbuf", [128, 192], "float32"), "sb": ("sbuf", [128, 192], "float32"), "z": ("sbuf", [128, 192], "float16"),
+    "st": ("sbuf", [128, 192], "float16"), "dpad": ("sbuf", [128, 192], "float32"), "db": ("sbuf", [128, 192], "float32"),
+    "uu": ("sbuf", [128, 96], "float32"), "tot": ("sbuf", [128, 32], "int32"), "nwv": ("sbuf", [128, 32], "int32"),
     "key": ("sbuf", [128, 8 * 16], "float32"), "cin": ("sbuf", [128, 6 * 16], "float32"),
-    "ks": ("sbuf", [128, 192], "float32"), "kl": ("sbuf", [128, 192], "float32"), "sl": ("sbuf", [128, 192], "float32"),
-    "yo": ("sbuf", [128, 6, 32], "float32"),
+    "sl": ("sbuf", [128, 16, 12], "float16"), "po": ("sbuf", [128, 192], "float16"),
+    "ks": ("sbuf", [128, 192], "float32"), "kl": ("sbuf", [128, 192], "float32"), "yo": ("sbuf", [128, 6, 32], "float32"),
     "pw0": ("psum", [128, 512], "float32"), "pw1": ("psum", [128, 512], "float32"),
     "pe0": ("psum", [128, 512], "float32"), "pe1": ("psum", [128, 512], "float32"),
-    "px0": ("psum", [128, 512], "float32"), "px1": ("psum", [128, 512], "float32"),
+    "ps0": ("psum", [128, 512], "float32"), "ps1": ("psum", [128, 512], "float32"),
     "pk0": ("psum", [128, 512], "float32"), "pk1": ("psum", [128, 512], "float32"),
 }
-PHASES = ["a", "i", "b", "c0", "c1", "c2", "c3", "c4", "c5", "s0", "s1", "k0", "k1", "y"]
-SEMAPHORES = (["cv", "cs", "ct", "cg", "sent", "dsa", "dsi", "dsb", "doa", "doi", "dob", "dla0", "dla1", "dla2", "dla3", "dls", "dlw", "dlb",
-               "dsy", "doy", "dya", "dys", "ara0", "ara1", "ara2", "ara3"]
-              + ["ar" + p for p in PHASES[1:]] + ["rl" + p for p in PHASES])
+PHASES = ["w", "a", "p", "c0", "c1", "c2", "c3", "c4", "c5", "s", "k0", "k1", "y0", "k2", "k3", "y1"]
+SEMAPHORES = (["cv", "cs", "ct", "cg", "sent", "dsa", "dsw", "dsr", "doa", "dow", "dlw", "dw0", "dw1", "dw2",
+               "dsy0", "dsy1", "doy", "dya", "dys", "ara0", "ara1"]
+              + ["ar" + p for p in PHASES if p != "a"] + ["rl" + p for p in PHASES])
 _PLAN = {}
+
+
+def slot(r):
+    return 2 * (r % 4) + r // 4
 
 
 def _bits(engines):
@@ -74,10 +78,11 @@ def make_plan(T, topo):
             best = (c, ring)
     ring = best[1]
     net = [ring.index(r) for r in range(N)]
-    calls, got = {}, {}
+    calls, got, order = {}, {}, []
 
     def add(src, ph, transfers):
-        calls.setdefault(src, {}).setdefault(ph, []).append(transfers)
+        if transfers:
+            calls.setdefault(src, {}).setdefault(ph, []).append(transfers)
         for dst, mask, sem, a, b in transfers:
             got[(dst, sem)] = got.get((dst, sem), 0) + bin(mask).count("1")
             got[(src, "sent")] = got.get((src, "sent"), 0) + bin(mask).count("1")
@@ -106,36 +111,52 @@ def make_plan(T, topo):
         off = topo.engines(c, cores[far[0]])
         loc = [e for e in on if e not in off]
 
-        def dram_phase(ph, ar, sname, lname, rname, sslot, lslot, k):
-            tr = []
-            for a in range(2):
-                for b in range(2):
-                    n = 2 * a + b
-                    tr.append((relay[a], _bits(loc[2 * n:2 * n + k]), "rl" + ph, (sname, sslot(pairs[a][b])), (rname, b)))
-            add(c, ph, tr)
-            tr = [(cores[far[b]], _bits(off[2 * b:2 * b + k]), ar, (sname, sslot(far[b])), (lname, lslot)) for b in range(2)]
-            tr.append((cores[sib[0]], _bits(off[4:4 + k]), ar, (sname, sslot(sib[0])), (lname, lslot)))
-            add(c, ph, tr)
+        def dram_phase(ph, ar, sname, lname, rname, sslot, lslot, k, to):
+            add(c, ph, [(relay[a], _bits(loc[4 * a + 2 * b:4 * a + 2 * b + k]), "rl" + ph, (sname, sslot(pairs[a][b])), (rname, b))
+                        for a in range(2) for b in range(2) if pairs[a][0] in to])
+            add(c, ph, [(cores[d], _bits(off[2 * b:2 * b + k]), ar, (sname, sslot(d)), (lname, lslot)) for b, d in enumerate(far + sib) if d in to])
             for a in range(2):
                 ro = topo.engines(relay[a], cores[pairs[a][0]])
                 pick = [ro[0:1], ro[4:5]] if k == 1 else [ro[0:4], ro[4:8]]
-                add(relay[a], ph, [(cores[pairs[a][b]], _bits(pick[b]), ar, (rname, b), (lname, lslot)) for b in range(2)])
+                if pairs[a][0] in to:
+                    add(relay[a], ph, [(cores[pairs[a][b]], _bits(pick[b]), ar, (rname, b), (lname, lslot)) for b in range(2)])
 
-        dram_phase("a", "ara%d" % (r // 2), "sa", "la", "ra", lambda d: net[d], r, 1)
-        dram_phase("i", "ari", "si", "li", "ri", lambda d: net[d], r, 2)
-        dram_phase("b", "arb", "sb", "lb", "rb", lambda d: net[d], r, 1)
-        dram_phase("y", "ary", "sy", "ly", "ry", lambda d: d, net[r], 2)
-        for n, (ph, sname, lname) in enumerate([("s0", "sx", "sl"), ("s1", "sx", "sl"), ("k0", "ks", "kl"), ("k1", "ks", "kl")]):
-            o = 96 * (n % 2)
-            land = (lname, o + 12 * net[r], 12)
-            tr = [(relay[a], _bits(on[8 * a:8 * a + 8]), "rl" + ph, (sname, o + 12 * pairs[a][0], 24), ("rk", 24 * n, 24)) for a in range(2)]
-            add(c, ph, tr)
-            tr = [(cores[far[b]], _bits(off[4 * b:4 * b + 4]), "ar" + ph, (sname, o + 12 * far[b], 12), land) for b in range(2)]
-            tr.append((cores[sib[0]], _bits(loc), "ar" + ph, (sname, o + 12 * sib[0], 12), land))
-            add(c, ph, tr)
+        def sbuf_phase(ph, sname, at, rname, ro_, land, n, to):
+            add(c, ph, [(relay[a], _bits(on[8 * a:8 * a + 8]), "rl" + ph, (sname, at(pairs[a][0]), 2 * n), (rname, ro_, 2 * n))
+                        for a in range(2) if pairs[a][0] in to])
+            add(c, ph, [(cores[d], _bits(off[4 * b:4 * b + 4] if b < 2 else loc), "ar" + ph, (sname, at(d), n), land)
+                        for b, d in enumerate(far + sib) if d in to])
             for a in range(2):
                 ro = topo.engines(relay[a], cores[pairs[a][0]])
-                add(relay[a], ph, [(cores[pairs[a][b]], _bits(ro[4 * b:4 * b + 4]), "ar" + ph, ("rk", 24 * n + 12 * b, 12), land) for b in range(2)])
+                if pairs[a][0] in to:
+                    add(relay[a], ph, [(cores[pairs[a][b]], _bits(ro[4 * b:4 * b + 4]), "ar" + ph, (rname, ro_ + n * b, n), land) for b in range(2)])
+
+        def half_phase(ph, sname, at, rname, ro_, land, n, to):
+            pair = [d for pr in pairs for d in pr if d in to]
+            add(c, ph, [(relay[b], _bits(on[8 * b:8 * b + 8]), "rl" + ph, (sname, at(d), n), (rname, ro_, n)) for b, d in enumerate(pair)])
+            add(c, ph, [(cores[d], _bits(off[4 * b:4 * b + 4] if b < 2 else on), "ar" + ph, (sname, at(d), n), land)
+                        for b, d in enumerate(far + sib) if d in to])
+            for b, d in enumerate(pair):
+                add(relay[b], ph, [(cores[d], topo.mask(relay[b], cores[d]), "ar" + ph, (rname, ro_, n), land)])
+
+        every = range(N)
+        order.append(pairs[0] + pairs[1] + far + sib + [r])
+        dram_phase("w", "arw", "sw", "lw", "rw", lambda d: net[d], r, 1, every)
+        land = ("va", 64 * r, 64)
+        add(c, "a", [(relay[a], _bits(loc[4 * a + 2 * b + 1:4 * a + 2 * b + 2]), "rla", ("sa", net[pairs[a][b]]), ("ra", b))
+                     for a in range(2) for b in range(2)])
+        add(c, "a", [(cores[d], _bits(e), "ara0", ("sa", net[d]), land) for d, e in zip(far + sib, (off[1:4:2], off[5:8:2], loc[0:3:2]))])
+        for a in range(2):
+            ro = topo.engines(relay[a], cores[pairs[a][0]])
+            add(relay[a], "a", [(cores[pairs[a][b]], _bits(ro[4 * b:4 * b + 4]), "ara1", ("ra", b), land) for b in range(2)])
+        sbuf_phase("p", "pq", lambda d: 24 * order[r].index(d), "rp", 0, ("px", 24 * r, 24), 24, every)
+        sbuf_phase("s", "px", lambda d: 24 * d, "rs", 0, ("sl", 2 * net[r], 2), 24, every)
+        for h in range(2):
+            half = range(4 * h, 4 * h + 4)
+            dram_phase("y%d" % h, "ary%d" % h, "sy", "ly", "ry", lambda d: d, net[r], 2, half)
+            for b in range(2):
+                n = 2 * h + b
+                half_phase("k%d" % n, "ks", lambda d: 48 * n + 12 * (d % 4), "rk", 12 * n, ("kl", 96 * b + 12 * net[r], 12), 12, half)
         d = ring[(net[r] - 1) % N]
         for n in range(6):
             ph = "c%d" % n
@@ -145,7 +166,7 @@ def make_plan(T, topo):
                 x = relay[0] if d in pairs[0] else relay[1]
                 add(c, ph, [(x, topo.mask(c, x), "rl" + ph, ("key", 16 * n, 16), ("rc", 16 * n, 16))])
                 add(x, ph, [(cores[d], topo.mask(x, cores[d]), "ar" + ph, ("rc", 16 * n, 16), ("cin", 16 * n, 16))])
-    return {"net": net, "calls": calls, "got": got}
+    return {"net": net, "order": order, "calls": calls, "got": got}
 
 
 def _side(T, s):
@@ -187,7 +208,7 @@ def arrange(ops):
             else:
                 hard.add(k)
                 d["need"] = True
-                order[k] = 2.2 if d["dma"] else (CFG["lag0"] if d["e"] == o["e"] else CFG["hop"] + (0.1 if d["e"] == "t" else 0.0))
+                order[k] = d["lag"] if d["dma"] else (CFG["lag0"] if d["e"] == o["e"] else CFG["hop"])
         if o["after"]:
             order[sent[o["after"][0]]] = o["after"][1]
         if o["rem"] and o["rem"] not in sent:
@@ -202,32 +223,88 @@ def arrange(ops):
             readers[x] = []
         for b in o["b"]:
             banks.setdefault(b, {})[o["e"]] = i
-    for i in range(len(ops) - 1, -1, -1):
-        o = ops[i]
-        o["level"] = o["c"] + max([ops[k]["level"] + ops[k]["order"][i] for k in o["succ"]] + [0.0])
-        o["left"], o["at"] = len(o["order"]), 0.0
-    ready = {e: [] for e in "vstgy"}
-    free = {e: 0.0 for e in "vstgy"}
+    return in_order(ops)
+
+
+def place_all(ops, pre, key, back):
+    n = len(ops)
+    key = list(key)
+    for i in (range(n - 1, -1, -1) if back else range(n)):
+        for k, lag in pre[i]:
+            if key[k] >= key[i]:
+                key[i] = key[k] + 1e-6
+    starts, ends = {e: [] for e in "vstgy"}, {e: [] for e in "vstgy"}
+    fin = [0.0] * n
+    for i in sorted(range(n), key=lambda x: key[x]):
+        t = 0.0
+        for k, lag in pre[i]:
+            if fin[k] + lag > t:
+                t = fin[k] + lag
+        e, c = ops[i]
+        st, en = starts[e], ends[e]
+        j = m = len(st)
+        while j and en[j - 1] > t + 1e-9:
+            j -= 1
+        while j < m and st[j] < t + c - 1e-9:
+            if en[j] > t:
+                t = en[j]
+            j += 1
+        st.insert(j, t)
+        en.insert(j, t + c)
+        fin[i] = t + c
+    return fin
+
+
+def in_order(ops):
+    n = len(ops)
+    ec = [(o["e"], o["c"]) for o in ops]
+    tail = [o["tail"] for o in ops]
+    pre = [list(o["order"].items()) for o in ops]
+    post = [[] for o in ops]
+    seen, names = {}, []
     for i, o in enumerate(ops):
-        if o["left"] == 0:
-            ready[o["e"]].append(i)
-    out = []
-    while len(out) < len(ops):
-        e = min((x for x in ready if ready[x]), key=lambda x: max(free[x], min(ops[k]["at"] for k in ready[x])))
-        now = max(free[e], min(ops[k]["at"] for k in ready[e]))
-        i = max((k for k in ready[e] if ops[k]["at"] <= now + CFG["la"][e]),
-                key=lambda k: (ops[k]["level"] + CFG["pri"].get(ops[k]["tag"] + e, 0.0), -k))
-        ready[e].remove(i)
-        o = ops[i]
-        free[e] = max(now, o["at"]) + o["c"]
-        out.append(i)
-        for k in o["succ"]:
-            s = ops[k]
-            s["at"] = max(s["at"], free[e] + s["order"][i])
-            s["left"] -= 1
-            if s["left"] == 0:
-                ready[s["e"]].append(k)
-    return out
+        name = (o["round"], o["tag"], o["e"])
+        seen[name] = seen.get(name, -1) + 1
+        names.append((name, seen[name]))
+        for k, lag in pre[i]:
+            post[k].append((i, lag))
+    state = [12345]
+
+    def rnd():
+        state[0] = (state[0] * 1103515245 + 12345) % 2147483648
+        return state[0] / 2147483648.0
+
+    def both(key):
+        one = place_all(ec, pre, key, False)
+        two = place_all(ec, pre, [-f for f in place_all(ec, post, [-f - t for f, t in zip(one, tail)], True)], False)
+        return min([(max(f + t for f, t in zip(fin, tail)), k, fin) for k, fin in enumerate((one, two))])
+
+    kind = "order"
+    if kind in _PLAN:
+        best = both([_PLAN[kind].get(x, 0.0) for x in names])
+    else:
+        key = [0.0] * n
+        for i in range(n - 1, -1, -1):
+            key[i] = min([key[k] - lag for k, lag in post[i]] + [-tail[i]]) - ec[i][1]
+        best = both(key)
+        for _ in range(CFG["tries"]):
+            lo, wide, size, whole = best[0] * rnd(), (2.0, 6.0, 12.0)[int(3 * rnd())], (0.2, 0.5, 1.5)[int(3 * rnd())], rnd() < 0.5
+            shift, key = {}, []
+            for i in range(n):
+                x = best[2][i] - ec[i][1]
+                if lo < x < lo + wide:
+                    if not whole:
+                        x += size * (rnd() - rnd())
+                    else:
+                        if names[i][0] not in shift:
+                            shift[names[i][0]] = 2 * size * (rnd() - rnd()) if rnd() < 0.3 else 0.0
+                        x += shift[names[i][0]]
+                key.append(x)
+            new = both(key)
+            if new[0] <= best[0]:
+                best = new
+        _PLAN[kind] = {names[i]: best[2][i] - ec[i][1] for i in range(n)}
+    return sorted(range(n), key=lambda i: (round(best[2][i] - ec[i][1], 7), i))
 
 
 def emit(g, T, ops):
@@ -278,25 +355,33 @@ def rank_program(g, core, T, topo):
                 g.wait_ge(T.sem["rl" + ph], got[(core, "rl" + ph)])
                 for tr in calls[ph]:
                     remote(g, core, T, topo, tr)
-        g.wait_ge(T.sem.sent, got[(core, "sent")])
-        return
-    me = plan["net"][rank]
-    cores = list(T.cores)
-    ops = []
-    tag = ["h"]
-    cyc, pe = CFG["cyc"], CFG["pe"]
+    else:
+        if "order" not in _PLAN:
+            arrange(rank_calls(g, T.cores[N - 1], N - 1, T, topo, plan))
+        emit(g, T, rank_calls(g, core, rank, T, topo, plan))
+    g.wait_ge(T.sem.sent, got[(core, "sent")])
 
-    def op(e, f, c, r=(), w=(), b=(), arr=None, dma=None, rem=None):
+
+def rank_calls(g, core, rank, T, topo, plan):
+    calls, got = plan["calls"][core], plan["got"]
+    me = plan["net"][rank]
+    ops = []
+    tag, now = ["h"], [-1, "A"]
+    cyc, pe, nd = CFG["cyc"], CFG["pe"], CFG["nd"]
+
+    def op(e, f, c, r=(), w=(), b=(), arr=None, dma=None, rem=None, lag=2.2):
         wait = [(arr[0], got[(core, arr[0])])] if arr else []
+        c = max(c, CFG["least"]) if e in "vs" and not dma else c
         ops.append({"e": e, "f": f, "c": c, "r": list(r), "w": list(w), "b": list(b), "wait": wait,
-                    "after": arr[1:] if arr else None, "dma": dma, "rem": rem, "tag": tag[0]})
+                    "after": arr[1:] if arr else None, "dma": dma, "rem": rem, "tag": now[1] + tag[0], "round": now[0], "lag": lag,
+                    "tail": lag if dma else CFG["tails"].get(rem, 0.0)})
 
     def send(ph, reads):
         for tr in calls[ph]:
             op("g", lambda q, tr=tr: remote(g, core, T, topo, tr), 0.3, r=reads, rem=ph)
 
-    def dma(e, sem, out, in_, r=(), w=(), arr=None):
-        op(e, lambda q: q.dma_start(out, in_), 0.05, r=r, w=w, arr=arr, dma=sem)
+    def dma(e, sem, out, in_, r=(), w=(), arr=None, lag=2.2):
+        op(e, lambda q: q.dma_start(out, in_), 0.05, r=r, w=w, arr=arr, dma=sem, lag=lag)
 
     def ts(n, out, in0, s1, s2, o0, o1, r, w, b=()):
         if o1 is None:
@@ -310,254 +395,410 @@ def rank_program(g, core, T, topo):
     def cp(n, out, in_, r, w, b=(), arr=None):
         op("v", lambda q: q.tensor_copy(out, in_), n * cyc, r, w, b, arr)
 
-    def scan(out, d0, d1, o0, o1, r, w, b=()):
-        op("v", lambda q: q.tensor_tensor_scan(out, d0, d1, 0.0, o0, o1), 96 * cyc, r, w, b)
+    def scan(n, out, d0, d1, o0, o1, r, w, b=(), arr=None):
+        op("v", lambda q: q.tensor_tensor_scan(out, d0, d1, 0.0, o0, o1), n * cyc, r, w, b, arr)
 
     def fill(n, ap, val, w):
         op("v", lambda q: q.memset(ap, val), n * cyc, (), w)
 
-    def mm(n, out, lhsT, rhs, start, stop, r, w, b):
-        op("t", lambda q: q.matmul(out, lhsT, rhs, start, stop), n * pe, r, w, b)
+    def mm(n, out, lhsT, rhs, start, stop, r, w, b, arr=None):
+        op("t", lambda q: q.matmul(out, lhsT, rhs, start, stop), n * pe, r, w, b, arr)
 
     def act(n, out, in_, r, w, b=()):
         op("s", lambda q: q.activation(out, in_, ACT.Copy), n * cyc, r, w, b)
 
-    PW, PE, PX, PK = [T.pw0, T.pw1], [T.pe0, T.pe1], [T.px0, T.px1], [T.pk0, T.pk1]
+    def iota(name, ap, pattern, base=0):
+        op("g", lambda q: q.iota(ap, pattern, base, -1, allow_small_or_imprecise_dtypes=True), 0.4, w=[name])
 
+    def pick(out, name, val, w, scale=None):
+        n = out.shape[1]
+        ts(64, out, T[name][:, 0:n], float(val), scale, ALU.is_equal, ALU.mult if scale else None, [name], w)
+
+    PW, PE, PK = [T.pw0, T.pw1], [T.pe0, T.pe1], [T.pk0, T.pk1]
+    XB = [(T.ps0, "ps0"), (T.ps1, "ps1"), (T.pe0, "pe0"), (T.pe1, "pe1")]
+    block = lambda t, k: t[:, 128 * k:128 * k + 128]
+
+    dma("s", "dsw", T.sw[:, 0:109, :], T.wt[:, 0:3052], w=["sw0"])
+    dma("y", "dsw", T.sw[:, 110:128, :], T.bs[:, 8:512], w=["sw1"])
+    dma("s", "dsw", T.sw[:, 109, 0:20], T.wt[:, 3052:3072], w=["sw2"])
+    dma("y", "dsw", T.sw[:, 109, 20:28], T.bs[:, 0:8], w=["sw3"])
+    dma("s", "dsr", T.ysr[:], T.sr[:], w=["ysr"])
     dma("y", "dsa", T.sa[:], T.a0[:], w=["sa"])
-    dma("s", "dsi", T.si[:, 0:64, :], T.sr[:], w=["si0"])
-    dma("s", "dsi", T.si[:, 64:128, :], T.wt[:], w=["si1"])
-    dma("s", "dsb", T.sb[:], T.bs[:], w=["sb"])
-    dma("y", "doa", T.la[rank], T.a0[16 * me:16 * me + 16, :], w=["la"])
-    dma("y", "doi", T.li[rank, 0:64, :], T.sr[16 * me:16 * me + 16, :], w=["li0"])
-    dma("y", "doi", T.li[rank, 64:128, :], T.wt[me:me + 1, :], w=["li1"])
-    dma("y", "dob", T.lb[rank], T.bs[me:me + 1, :], w=["lb"])
-    op("g", lambda q: q.iota(T.kc[:, 0:1], [[0, 1]], 0, 1), 0.14, w=["kc0"])
-    op("g", lambda q: q.iota(T.mlo[:], [[0, 8], [1, 16]], 0, 0, allow_small_or_imprecise_dtypes=True), 0.4, w=["mlo"])
-    op("g", lambda q: q.iota(T.mhi[:], [[1, 8], [0, 16]], 0, 0, allow_small_or_imprecise_dtypes=True), 0.4, w=["mhi"])
+    dma("y", "doa", T.va[:, 64 * rank:64 * rank + 64], T.a0[16 * me:16 * me + 16, :], w=["va"])
+    op("y", lambda q: q.dma_start(T.lw[rank], T.sw[me]), 0.05, ["sw0", "sw1", "sw2", "sw3"], ["lw"], dma="dow")
+    iota("jz", T.jz[:], [[16, 8], [-200, 2], [1, 16]], 200)
+    iota("jr", T.jr[:], [[0, 8], [8, 16]])
+    iota("jd", T.jd[:], [[1, 128]])
+    iota("jb", T.jb[:], [[16, 8]])
+    send("w", ["sw0", "sw1", "sw2", "sw3"])
     send("a", ["sa"])
-    send("i", ["si0", "si1"])
-    send("b", ["sb"])
-    blocks = sorted(range(4), key=lambda k: (k != rank // 2, not topo.may_write(cores[2 * k], core)))
-    for n, k in enumerate(blocks):
-        dma("y", "dla%d" % k, T.vsb[32 * k:32 * k + 32, :], T.la[2 * k:2 * k + 2], r=["la"], w=["va%d" % k],
-            arr=("ara%d" % k, "a", 4.5 if n < 2 else 8.0))
-    dma("y", "dls", T.ysr[:], T.li[:, 0:64, :], r=["li0"], w=["ysr"], arr=("ari", "i", 6.5))
-    dma("y", "dlw", T.wi[:], T.li[:, 64:128, :], r=["li1"], w=["wi"])
-    fill(256, T.bi[:], 0, ["bi0", "bi1"])
-    for h in range(2):
-        dma("y", "dlb", T.bi[h::16, :], T.lb[:, 64 * h:64 * h + 64, :], r=["lb"], w=["bi%d" % h], arr=("arb", "b", 6.0))
-    fill(96, T.dmax[:], 1.0, ["dmax"])
-    fill(96, T.dmin[:], -1.0, ["dmin"])
-    fill(96, T.keep[:], 1.0, ["keep"])
-    fill(192, T.fpad[:], -1.0, ["fpad0", "fpad1"])
-    fill(192, T.dpad[:], -4096.0, ["dpad0", "dpad1"])
-    fill(64, T.coef[:, 0:16], 104.0, ["coefa"])
-    fill(64, T.coef[:, 16:32], 56.0, ["coefb"])
-    fill(192, T.bc[:], 0.0, ["bc0", "bc1"])
-    for s in range(D):
-        fill(64, T.coff[:, s::6], float(4096 * (5 - s) + 2048), ["coff%d" % s])
-    coff = ["coff%d" % s for s in range(D)]
-    fill(64, T.dmax[:, 0::6], -BIG, ["dmax"])
-    fill(64, T.dmin[:, 0::6], BIG, ["dmin"])
-    fill(64, T.keep[:, 0::6], 0.0, ["keep"])
-    cp(192, T.zz[:, 0:192], T.bc[:, 0:192], ["bc0", "bc1"], ["zza"])
-    cp(80, T.zz[:, 192:272], T.bc[:, 0:80], ["bc0", "bc1"], ["zzb"])
-    ts(64, T.kc[:, 1:2], T.kc[:, 0:1], 4, None, ALU.arith_shift_right, None, ["kc0"], ["kc1"])
-    ts(64, T.kc[:, 2:3], T.kc[:, 0:1], 15, None, ALU.bitwise_and, None, ["kc0"], ["kc2"])
-    cp(64, T.kf[:], T.kc[:, 1:3], ["kc1", "kc2"], ["kf"])
-    ts(128, T.d16[:], T.mlo[:], T.kf[:, 1:2], None, ALU.is_equal, None, ["mlo", "kf"], ["d16"])
-    ts(64, T.rm8[:], T.mlo[:, 0:8], T.kf[:, 0:1], None, ALU.is_equal, None, ["mlo", "kf"], ["rm8"])
-    ts(128, T.blk[:], T.mhi[:], T.kf[:, 0:1], None, ALU.is_equal, None, ["mhi", "kf"], ["blk"])
-    for j in range(8):
-        ts(128, T.rep[:, 128 * j:128 * j + 128], T.d16[:], T.rm8[:, j:j + 1], None, ALU.mult, None, ["d16", "rm8"], ["rep%d" % j])
-    for j in range(8):
-        ts(64, T.zz[:, 16 + 32 * j:32 + 32 * j], T.d16[:, 0:16], T.rm8[:, j:j + 1], None, ALU.mult, None, ["d16", "rm8", "zza", "zzb"], ["zz%d" % j])
-    tt(256, T.idh[:], T.d16[:], T.blk[:], ALU.mult, ["d16", "blk"], ["idh"])
-    tt(256, T.idb[:], T.d16[:], T.blk[:], ALU.mult, ["d16", "blk"], ["idb"])
-    ts(64, T.b8[:], T.rm8[:], 8.0, None, ALU.mult, None, ["rm8"], ["b8"])
-    for c in range(16):
-        ts(128, T.sel[:, 128 * c:128 * c + 128], T.blk[:], T.d16[:, c:c + 1], None, ALU.mult, None, ["d16", "blk"], ["sel%d" % c])
+    dma("y", "dlw", T.wi[0:112, :], T.lw[:], r=["lw"], w=["wi"], arr=("arw", "w", CFG["tw"]))
+    ts(128, T.zz[:], T.jz[:], 0.0, None, ALU.is_equal, None, ["jz"], ["zz"])
 
-    winall = lambda u: ["win%d_%d_%d" % (u, j, h) for j in range(8) for h in range(2)]
-    vall = ["v0", "v1", "v2", "v3"]
+    def place(out, a, rhs, n, r, w, b, arr=None):
+        mm(32, out(32), T.zz[:, 32 * a:32 * a + 32], rhs(1), True, False, r + ["zz"], w, b, arr)
+        mm(max(16, n), out(16), T.zz[:, 32 * a + 16:32 * a + 32], rhs(0), False, True, r + ["zz"], w, b)
 
-    rot = [(T.pe0, "pe0"), (T.pe1, "pe1"), (T.px0, "px0"), (T.px1, "px1"), (T.pk0, "pk0"), (T.pk1, "pk1"), (T.pw0, "pw0"), (T.pw1, "pw1")]
-    for n, j in enumerate([2 * k + i for k in blocks for i in range(2)]):
-        k = j // 2
-        ps, bank = rot[n]
-        mm(512, ps[:], T.rep[32 * k:32 * k + 32, 128 * j:128 * j + 128], T.vsb[32 * k:32 * k + 32, :], True, True,
-           ["rep%d" % j, "va%d" % k], ["first%d" % j], [bank])
-        (act if n % 2 else cp)(512, T.win[:, 512 * j:512 * j + 512], ps[:], ["first%d" % j], ["win0_%d_0" % j, "win0_%d_1" % j], [bank])
-    for qq in range(4):
-        cp(64, T.off[:, 48 * qq:48 * qq + 48], T.ysr[:, :, 8 * qq:8 * qq + 8], ["ysr"], ["off%d" % qq])
-    cp(192, T.wf[:], T.wi[:], ["wi"], ["wf"])
-    cp(256, T.bf[:], T.bi[:], ["bi0", "bi1"], ["bf"])
-    cp(192, T.wq[:], T.wf[:], ["wf"], ["wq"])
-    cp(256, T.bq[:], T.bf[:], ["bf"], ["bq"])
-
-    def place(out, a, rhs, r, w, b):
-        mm(32, out(32), T.zz[:, 32 * a:32 * a + 32], rhs(1), True, False, r + ["zz%d" % a], w, b)
-        mm(16, out(16), T.zz[:, 32 * a + 16:32 * a + 32], rhs(0), False, True, r + ["zz%d" % a], w, b)
-
-    def first_sources(h):
-        a = 96 * h
-        cp(96, T.bc[:, a:a + 96], T.off[:, a:a + 96], ["off%d" % (2 * h), "off%d" % (2 * h + 1)], ["bc%d" % h])
-        ts(96, T.py[:, a:a + 96], T.bc[:, a:a + 96], -2048.0, None, ALU.add, None, ["bc%d" % h], ["py%d" % h])
-        for j in range(8):
+    tag[0] = "i"
+    for q in range(4):
+        ts(64, T.py[:, 48 * q:48 * q + 48], T.ysr[:, :, 8 * q:8 * q + 8], -2048.0, None, ALU.add, None, ["ysr"], ["py%d" % q])
+    order = plan["order"][rank]
+    for k in range(2):
+        for c, d in enumerate(order[4 * k:4 * k + 4]):
             for n in range(4):
-                place(lambda m: PK[h][32 * n:32 * n + m, 128 + 12 * j:140 + 12 * j], j,
-                      lambda lo: T.py[:, a + 2 * n + lo:a + 96:8], ["py%d" % h], ["cv%d" % h], ["pk%d" % h])
-        cp(96, T.px[:, a:a + 96], PK[h][:, 128:224], ["cv%d" % h], ["px%d" % h], ["pk%d" % h])
-        tt(96, T.sx[:, a:a + 96], PK[h][:, 128:224], T.coff[:], ALU.add, ["cv%d" % h] + coff, ["sx%d" % h], ["pk%d" % h])
+                place(lambda m: PK[k][32 * n:32 * n + m, 24 * c:24 * c + 24], plan["net"][d],
+                      lambda lo: T.py[:, 2 * n + lo::8], 24, ["py%d" % q for q in range(4)], ["cv%d" % k], ["pk%d" % k])
+        cp(96, T.pq[:, 96 * k:96 * k + 96], PK[k][:, 0:96], ["cv%d" % k], ["pq%d" % k], ["pk%d" % k])
+        op("g", lambda q, k=k: remote(g, core, T, topo, calls["p"][k]), 0.3, r=["pq%d" % k], rem="p")
+    cp(64, T.px[:, 24 * rank:24 * rank + 24], T.pq[:, 168:192], ["pq1"], ["px0", "px1"])
+    iota("jw", T.jw[:], [[14, 4], [1, 2], [0, 16]])
+    iota("ja", T.ja[:], [[0, 8], [1, 16]])
+    for c in range(8):
+        pick(block(T.rep, 8 + c), "jr", -c, ["rep%d" % (8 + c)])
 
-    def gather(q, k, eng, u):
-        tag[0] = "g%d" % q
-        c = 768 * q + 384 * k
-        src = lambda: T.win[:, W * u:W * u + W].indirect(T.off[:, 48 * q + 24 * k:48 * q + 24 * k + 24])
-        r, w, cost = winall(u) + ["off%d" % q], ["p%d_%d" % (q, k)], 0.06 + 384 * CFG["gc"] * cyc
-        if eng == "s":
-            op("s", lambda e: e.activation(T.p[:, c:c + 384], src(), ACT.Copy), cost, r, w)
+    tag[0] = "h"
+    for j in range(8):
+        pick(block(T.rep, j), "ja", -16 * j, ["rep%d" % j])
+    for name, scale in (("idh", None), ("idb", None), ("i104", 104.0)) + (() if CFG["uuv"] else (("idf", None), ("i56", 56.0))):
+        pick(T[name][:], "jd", 0, [name], scale)
+    for h in range(2):
+        for s in range(D + 1):
+            pick(block(T.sel, 7 * h + s), "jw", -56 * h - 2 * s, ["sel%d" % (7 * h + s)])
+    ts(64, T.b8[:, 8:16], T.jb[:], -16.0, None, ALU.is_gt, None, ["jb"], ["b8a"])
+    ts(64, T.b8[:, 16:24], T.jb[:], 0.0, 8.0, ALU.is_le, ALU.mult, ["jb"], ["b8b"])
+    tt(64, T.b8[:, 0:8], T.b8[:, 8:16], T.b8[:, 16:24], ALU.mult, ["b8a", "b8b"], ["b8"])
+    if nd:
+        iota("jp", T.jp[:], [[1, 16], [16, 8]])
+        iota("jq", T.jq[:], [[1, 8], [8, 16]])
+        iota("jv", T.jv[:], [[0, 16], [14, 4], [1, 2]])
+        pick(T.turn[:], "jp", 0, ["turn"])
+        pick(T.unturn[:], "jq", 0, ["unturn"])
+        pick(block(T.sel, 14), "jv", -12, ["sel14"])
+    for name, val, first, at in (("dmax", 1.0, -BIG, 0), ("dmin", -1.0, BIG, 0), ("drev", 1.0, BIG, 5), ("keep", 1.0, 0.0, 0)):
+        fill(96, T[name][:], val, [name])
+        fill(64, T[name][:, at::6], first, [name])
+    cp(96, T.keeph[:], T.keep[:], ["keep"], ["keeph"])
+    fill(192, T.dpad[:], 0.0, ["dpad0", "dpad1"])
+    fill(64, T.top[:], 255.0, ["top"])
+    for s in range(D):
+        fill(64, T.coff[:, s:96:6], float(4096 * (6 - s)), ["coff%d" % s])
+    fill(64, T.coff[:, 96:112], 2048.0, ["coff6"])
+    cp(112, T.coffh[:], T.coff[:], ["coff%d" % s for s in range(D + 1)], ["coffh"])
+
+    part = lambda u, h, jj: ["win%d_%d_%d_%d" % (u, h, j, b) for j in (2 * jj, 2 * jj + 1) for b in range(4)]
+    bydma = lambda u: ["wd%d_%d" % (u, j) for j in range(8)]
+    winall = lambda u: [x for h in range(2) for jj in range(4) for x in part(u, h, jj)] + bydma(u)
+    vall = ["v%d" % i for i in range(8)]
+
+    tag[0] = "f"
+    for n, r in enumerate(order[::-1]):
+        ps, bank = XB[n % 4]
+        for c in range(8):
+            mm(64, ps[:, 64 * c:64 * c + 64], block(T.rep, 8 + c), T.va[:, 64 * r:64 * r + 64], True, True,
+               ["rep%d" % (8 + c), "va"], [bank], [bank], ("ara%d" % (n // 4), "a", CFG["ta"][n // 4]))
+        (cp if n in CFG["vfirst"] else act)(512, T.win[:, 512 * r:512 * r + 512], ps[:], [bank], part(0, r // 4, r % 4), [bank])
+    tag[0] = "w"
+    ts(256, T.wq[0:112, :], T.wi[0:112, :], 0.0, None, ALU.add, None, ["wi"], ["wq"])
+
+    def keyed(h, px, name):
+        H = str(h)
+        tag[0] = "x" + H
+        mm(96, PK[h][:, 192:288], T.i104[:], px[:, 96 * h:96 * h + 96], True, False, ["i104", name + H], ["sx" + H], ["pk" + H])
+        mm(96, PK[h][:, 192:288], T.i104[:], T.coffh[:, 0:96], False, True, ["i104", "coffh"], ["sx" + H], ["pk" + H])
+
+    def lists(h, more=True, arr=None):
+        H = str(h)
+        a = 96 * h
+        tag[0] = "l" + H
+        for n in range(8):
+            for jj in range(4):
+                place(lambda m: PK[h][32 * jj:32 * jj + m, 416 + n:512:8], n,
+                      lambda lo: T.px[:, a + 12 * (2 * jj + lo):a + 12 * (2 * jj + lo) + 12], 12, ["px" + H], ["cv" + H], ["pk" + H], arr)
+        ts(96, T.off[:, a:a + 96], PK[h][:, 416:512], 2048.0, None, ALU.add, None, ["cv" + H], ["off" + H], ["pk" + H])
+        if more:
+            keyed(h, T.px, "px")
+
+    for h in range(2):
+        lists(h, True, ("arp", "p", CFG["tp"]))
+
+    def sources(i, u):
+        return T.win[:, W * u:W * u + W].indirect(T.off[:, 24 * i:24 * i + 24])
+
+    def gather(i, u):
+        tag[0] = "g%d" % i
+        op("s", lambda e: e.activation(T.p[:, 384 * i:384 * i + 384], sources(i, u), ACT.Copy), 0.06 + 384 * CFG["gc"] * cyc,
+           winall(u) + ["off%d" % (i // 4)], ["p%d" % i])
+
+    def sums(i, t, turned):
+        k, I, a, h = i % 2, str(i), 384 * i, i // 4
+        tag[0] = "w" + I
+        ps, bank = XB[CFG["xbank"][i]]
+        wb, xb, out = ["pw%d" % k], [bank], ps[:, 0:64]
+        wq = T.wq[0:112, 64 * (i % 4):64 * (i % 4) + 64]
+        sel = lambda c: T.sel[0:112, 128 * c:128 * c + 128]
+        fused = i in CFG["fused"]
+        kept = T.wk[:, 384 * h:384 * h + 384]
+        if t == 0 or not fused:
+            for s in range(D):
+                mm(64, PW[k][:, 64 * s:64 * s + 64], sel(7 * h + s), wq, True, True, ["wq", "sel%d" % (7 * h + s)], wb, wb)
+        tag[0] = "m" + I
+        if fused and t > 0:
+            op("v", lambda q: q.tensor_tensor(T.pw[:, a:a + 384], sources(i, t % 2), kept, ALU.mult), 0.05 + 384 * CFG["gc"] * cyc,
+               winall(t % 2) + ["off%d" % (2 * h + k), "wk" + I], ["m" + I])
         else:
-            op("v", lambda e: e.tensor_copy(T.p[:, c:c + 384], src()), cost, r, w)
+            tt(384, T.pw[:, a:a + 384], T.p[:, a:a + 384], PW[k][:, 0:384], ALU.mult, ["p" + I] + wb, ["m" + I], wb)
+        if fused and t == 0:
+            tag[0] = "k" + I
+            act(384, kept, PW[k][:, 0:384], wb, ["wk" + I], wb)
+            tag[0] = "m" + I
+        c, there, back = (14, "turn", "unturn") if turned else (7 * h + 6, "idh", "idb")
+        if i in CFG["second"]:
+            mm(64, out, sel(7 * h + 6), wq, True, False, ["wq", "sel%d" % (7 * h + 6)], xb, xb)
+            for s in range(D):
+                mm(64, out, T.idh[:], T.pw[:, a + 64 * s:a + 64 * s + 64], False, s == 5, ["idh", "m" + I], xb, xb)
+            tag[0] = "n" + I
+            ts(64, out, out, 0.0, 255.0, ALU.max, ALU.min, xb, xb, xb)
+            tag[0] = "a" + I
+            ps, bank = XB[CFG["second"][i]]
+            xb, two = [bank], ps[:, 0:64]
+            mm(64, two, sel(c), wq, True, False, ["wq", "sel%d" % c], xb, xb)
+            for s in range(D):
+                mm(64, two, T[there][:], T.pw[:, a + 64 * s:a + 64 * s + 64], False, s == 5, [there, "m" + I], xb, xb)
+            op("s", lambda q: q.activation(two, two, ACT.Relu, T.top[:], -1.0), 64 * cyc, xb + ["top"], xb, xb)
+            op("s", lambda q: q.activation(T.vsb[:, 64 * i:64 * i + 64], two, ACT.Relu, T.top[:], -1.0), 64 * cyc, xb + ["top"], ["v" + I], xb)
+            return
+        mm(64, out, sel(c), wq, True, False, ["wq", "sel%d" % c], xb, xb)
+        for s in range(D):
+            mm(64, out, T[there][:], T.pw[:, a + 64 * s:a + 64 * s + 64], False, s == 5, [there, "m" + I], xb, xb)
+        tag[0] = "n" + I
+        if i in CFG["aclamp"]:
+            op("s", lambda q: q.activation(out, out, ACT.Relu, T.top[:], -1.0), 64 * cyc, xb + ["top"], xb, xb)
+            op("s", lambda q: q.activation(T.vsb[:, 64 * i:64 * i + 64], out, ACT.Relu, T.top[:], -1.0), 64 * cyc, xb + ["top"], ["v" + I], xb)
+        else:
+            ts(64, T.vsb[:, 64 * i:64 * i + 64], out, 0.0, 255.0, ALU.max, ALU.min, xb, ["v" + I], xb)
+        if i in CFG["twice"] and not turned:
+            ts(64, out, out, 0.0, 255.0, ALU.max, ALU.min, xb, xb, xb)
+        else:
+            mm(64, out, T[back][:], T.vsb[:, 64 * i:64 * i + 64], True, True, [back, "v" + I], xb, xb)
 
-    def sums(q, k):
+    def products(i, final):
+        k, q = i % 2, i // 2
         h, b = q // 2, q % 2
-        tag[0] = "m%d" % q
-        for s in range(3 * k, 3 * k + 3):
-            e0 = 512 * s + 128 * q
-            e = e0
-            while e < e0 + 128:
-                c = e // 192
-                n = min(e0 + 128, 192 * (c + 1)) - e
-                o = 128 * (s - 3 * k) + e - e0
-                mm(n, PW[k][:, o:o + n], T.sel[:, 128 * c:128 * c + 128], T.wq[:, e - 192 * c:e - 192 * c + n], True, True,
-                   ["wq", "sel%d" % c], ["pw%d" % k], ["pw%d" % k])
-                e += n
-        c = 768 * q + 384 * k
-        tt(384, T.pw[:, c:c + 384], T.p[:, c:c + 384], PW[k][:, 0:384], ALU.mult, ["p%d_%d" % (q, k), "pw%d" % k], ["m%d_%d" % (q, k)], ["pw%d" % k])
-        out = PX[b][:, 0:128]
-        if k == 0:
-            mm(128, out, T.sel[:, 128 * h:128 * h + 128], T.bq[:, 128 * b:128 * b + 128], True, False, ["bq", "sel%d" % h], ["x%d" % b], ["px%d" % b])
-        for s in range(3 * k, 3 * k + 3):
-            c = 768 * q + 128 * s
-            mm(128, out, T.idh[:], T.pw[:, c:c + 128], False, s == 5, ["idh", "m%d_%d" % (q, k)], ["x%d" % b], ["px%d" % b])
-
-    def clamp(q):
-        b, c = q % 2, 128 * q
-        ts(128, T.vsb[:, c:c + 128], PX[b][:, 0:128], 0.0, 255.0, ALU.max, ALU.min, ["x%d" % b], ["v%d" % q, "va0", "va1", "va2", "va3"], ["px%d" % b])
-        mm(128, PX[b][:, 0:128], T.idb[:], T.vsb[:, c:c + 128], True, True, ["idb", "v%d" % q], ["x%d" % b], ["px%d" % b])
-
-    def spread(h, u):
-        tag[0] = "e%d" % h
-        for jj in range(4):
-            bank = ["pe%d" % (jj % 2)]
-            for j in (2 * jj, 2 * jj + 1):
-                mm(256, PE[jj % 2][:, 256 * (j % 2):256 * (j % 2) + 256], T.rep[:, 128 * j:128 * j + 128], T.vsb[:, 256 * h:256 * h + 256],
-                   True, True, ["v%d" % (2 * h), "v%d" % (2 * h + 1), "rep%d" % j], bank, bank)
-            for j in (2 * jj, 2 * jj + 1):
-                act(256, T.win[:, W * u + 512 * j + 256 * h:W * u + 512 * j + 256 * h + 256], PE[jj % 2][:, 256 * (j % 2):256 * (j % 2) + 256],
-                    bank, ["win%d_%d_%d" % (u, j, h)], bank)
-
-    def scores(q):
-        h, b = q // 2, q % 2
-        tag[0] = "v%d" % q
+        tag[0] = "v%d" % i
+        ps, bank = XB[CFG["xbank"][i]]
         for s in range(D):
             c = 768 * q + 128 * s
-            tt(128, T.pv[:, c:c + 128], T.p[:, c:c + 128], PX[b][:, 0:128], ALU.mult,
-               ["p%d_%d" % (q, s // 3), "x%d" % b], ["pv%d_%d" % (q, s)], ["px%d" % b])
-            mm(256, PK[h][:, 6 * b + s:96:12], T.pv[:, c:c + 128], T.b8[:], True, True, ["pv%d_%d" % (q, s), "b8"], ["k%d" % h], ["pk%d" % h])
+            tt(64, T.pv[:, c + 64 * k:c + 64 * k + 64], T.p[:, 384 * i + 64 * s:384 * i + 64 * s + 64], ps[:, 0:64], ALU.mult,
+               ["p%d" % i, bank], ["pv%d_%d" % (i, s)], [bank])
+            if k:
+                out = PK[h][:, 48 * b + s:48 * b + 48:6] if final else PK[h][:, 6 * b + s:96:12]
+                mm(256, out, T.pv[:, c:c + 128], T.b8[:, 0:8], True, True,
+                   ["pv%d_%d" % (i - 1, s), "pv%d_%d" % (i, s), "b8"], ["k%d" % h], ["pk%d" % h])
+        if final and k:
+            tag[0] = "t%d" % h
+            act(64, T.ks[:, 48 * q:48 * q + 48], PK[h][:, 48 * b:48 * b + 48], ["k%d" % h], ["ks%d" % q], ["pk%d" % h])
+            send("k%d" % q, ["ks%d" % q])
+            if rank // 4 == h:
+                c = 48 * q + 12 * (rank % 4)
+                act(64, T.kl[:, 96 * b + 12 * me:96 * b + 12 * me + 12], T.ks[:, c:c + 12], ["ks%d" % q], ["kl%d" % b])
 
-    def renew(h, slot, own):
+    def sums(i, t, turned):
+        q, k, I, a, h = i // 2, i % 2, str(i), 384 * i, i // 4
+        tag[0] = "w" + I
+        ps, bank = XB[CFG["xbank"][q]]
+        wb, xb, out = ["pw%d" % k], [bank], ps[:, 0:128]
+        wq = T.wq[0:112, 128 * (q % 2):128 * (q % 2) + 128]
+        sel = lambda c: T.sel[0:112, 128 * c:128 * c + 128]
+        fused = i in CFG["fused"]
+        kept = T.wk[:, 384 * q:384 * q + 384]
+        if t == 0 or not fused:
+            for s in range(3):
+                c = 7 * h + 3 * k + s
+                mm(128, PW[k][:, 128 * s:128 * s + 128], sel(c), wq, True, True, ["wq", "sel%d" % c], wb, wb)
+        tag[0] = "m" + I
+        if fused and t > 0:
+            op("v", lambda e: e.tensor_tensor(T.pw[:, a:a + 384], sources(i, t % 2), kept, ALU.mult), 0.05 + 384 * CFG["gc"] * cyc,
+               winall(t % 2) + ["off%d" % h, "wk" + I], ["m" + I])
+        else:
+            tt(384, T.pw[:, a:a + 384], T.p[:, a:a + 384], PW[k][:, 0:384], ALU.mult, ["p" + I] + wb, ["m" + I], wb)
+        if fused and t == 0:
+            tag[0] = "k" + I
+            act(384, kept, PW[k][:, 0:384], wb, ["wk" + I], wb)
+            tag[0] = "m" + I
+        c, there, back = (14, "turn", "unturn") if turned else (7 * h + 6, "idh", "idb")
+        if k == 0:
+            mm(128, out, sel(c), wq, True, False, ["wq", "sel%d" % c], xb, xb)
+        for s in range(3):
+            mm(128, out, T[there][:], T.pw[:, a + 128 * s:a + 128 * s + 128], False, k == 1 and s == 2, [there, "m" + I], xb, xb)
+        if k == 1:
+            tag[0] = "n%d" % q
+            v, names = T.vsb[:, 128 * q:128 * q + 128], vall[2 * q:2 * q + 2]
+            if q in CFG["aclamp"]:
+                op("s", lambda e: e.activation(out, out, ACT.Relu, T.top[:], -1.0), 128 * cyc, xb + ["top"], xb, xb)
+                op("s", lambda e: e.activation(v, out, ACT.Relu, T.top[:], -1.0), 128 * cyc, xb + ["top"], names, xb)
+            else:
+                ts(128, v, out, 0.0, 255.0, ALU.max, ALU.min, xb, names, xb)
+            if q in CFG["twice"] and not turned:
+                ts(128, out, out, 0.0, 255.0, ALU.max, ALU.min, xb, xb, xb)
+            else:
+                mm(128, out, T[back][:], v, True, True, [back] + names, xb, xb)
+
+    def products(q, final):
+        h, b = q // 2, q % 2
+        tag[0] = "v%d" % q
+        ps, bank = XB[CFG["xbank"][q]]
+        for s in range(D):
+            c = 768 * q + 128 * s
+            tt(128, T.pv[:, c:c + 128], T.p[:, c:c + 128], ps[:, 0:128], ALU.mult, ["p%d" % (2 * q + s // 3), bank], ["pv%d_%d" % (q, s)], [bank])
+            out = PK[h][:, 48 * b + s:48 * b + 48:6] if final else PK[h][:, 6 * b + s:96:12]
+            mm(256, out, T.pv[:, c:c + 128], T.b8[:, 0:8], True, True, ["pv%d_%d" % (q, s), "b8"], ["k%d" % h], ["pk%d" % h])
+        if final:
+            tag[0] = "t%d" % h
+            act(64, T.ks[:, 48 * q:48 * q + 48], PK[h][:, 48 * b:48 * b + 48], ["k%d" % h], ["ks%d" % q], ["pk%d" % h])
+            send("k%d" % q, ["ks%d" % q])
+            if rank // 4 == h:
+                c = 48 * q + 12 * (rank % 4)
+                act(64, T.kl[:, 96 * b + 12 * me:96 * b + 12 * me + 12], T.ks[:, c:c + 12], ["ks%d" % q], ["kl%d" % b])
+
+    def spread_dma(t, groups, after, lag):
+        u = (t + 1) % 2
+        for j in groups:
+            dma("y", "dw%d" % t, T.win[16 * j:16 * j + 16, W * u:W * u + 256 * nd], T.vsb[0:16 * nd, 0:256], vall[0:4] + after,
+                [bydma(u)[j]] + [x for jj in range(nd // 2) for x in part(u, 0, jj)], lag=lag)
+
+    def spread(h, t):
+        u = (t + 1) % 2
+        tag[0] = "e%d" % h
+        first = nd // 2 if h == 0 else 0
+        if first:
+            spread_dma(t, range(CFG["early"]), [], CFG["td"][0])
+        if h == 1 and CFG["fine"]:
+            for b, (i, m) in enumerate(CFG["fine"]):
+                tag[0] = "e%d" % (2 + b)
+                n = 64 * m
+                for k in range(2):
+                    bank = ["pe%d" % k]
+                    for j in range(4 * k, 4 * k + 4):
+                        mm(n, PE[k][:, n * (j % 4):n * (j % 4) + n], block(T.rep, j), T.vsb[:, 64 * i:64 * i + n],
+                           True, True, vall[i:i + m] + ["rep%d" % j], bank, bank)
+                    for j in range(4 * k, 4 * k + 4):
+                        c = W * u + 2048 + 256 * j + 64 * (i - 4)
+                        act(n, T.win[:, c:c + n], PE[k][:, n * (j % 4):n * (j % 4) + n], bank,
+                            ["win%d_1_%d_%d" % (u, j, x % 4) for x in range(i, i + m)], bank)
+            return
+        for jj in range(first, 4):
+            bank = ["pe%d" % (jj % 2)]
+            for j in (2 * jj, 2 * jj + 1):
+                c = 4 + j if first else j
+                mm(256, PE[jj % 2][:, 256 * (j % 2):256 * (j % 2) + 256], block(T.rep, c), T.vsb[:, 256 * h:256 * h + 256],
+                   True, True, vall[4 * h:4 * h + 4] + ["rep%d" % c], bank, bank)
+            c = W * u + 2048 * h + 512 * jj
+            (cp if (h, jj) in CFG["vspread"] else act)(512, T.win[:, c:c + 512], PE[jj % 2][:], bank, part(u, h, jj), bank)
+
+    def renew(h, sl, own):
         H = str(h)
         tag[0] = "t" + H
         a, z = 96 * h, 16 * h
-        K, kb = PK[h][:, 0:96], ["pk" + H]
+        kb = ["pk" + H]
         c96 = lambda t: t[:, a:a + 96]
         c16 = lambda t: t[:, z:z + 16]
-        last = lambda t: t[:, a + 5:a + 96:6]
-        sx, sxn, keyn = (T.sl if own else T.sx), ("sl" if own else "sx") + H, "key%d" % slot
-        scan(c96(T.scb), T.dmax[:], K, ALU.add, ALU.max, ["dmax", "k" + H], ["scb" + H], kb)
-        scan(c96(T.scw), T.dmin[:], K, ALU.add, ALU.min, ["dmin", "k" + H], ["scw" + H], kb)
-        cp(64, T.key[:, 16 * slot:16 * slot + 16], last(T.scb), ["scb" + H], [keyn])
+        back = lambda t, o: t[:, o + 95:o - 1 if o else None:-1]
+        last = lambda t, o: t[:, o + 5:o + 96:6]
+        ew, sx = PK[h][:, 96:192], PK[h][:, 192:288]
+        if own:
+            n = 2 * (rank // 4) + h
+            K, kn, arr = c96(T.kl), "kl" + H, ("ark%d" % n, "k%d" % n, CFG["tk"])
+            scb, so, bc, bo, src, pxn = PK[h], 0, PK[h], 320, T.po, "po" + H
+        else:
+            K, kn, arr = PK[h][:, 0:96], "k" + H, None
+            scb, so, bc, bo, src, pxn = T.scb, a, T.bc, a, T.px, "px" + H
+        keyn, px = "key%d" % sl, c96(src)
+        scan(96, scb[:, so:so + 96], T.dmax[:], K, ALU.add, ALU.max, ["dmax", kn], ["scb" + H], kb, arr)
+        cp(64, T.key[:, 16 * sl:16 * sl + 16], last(scb, so), ["scb" + H], [keyn], kb if own else [])
         if not own:
-            send("c%d" % slot, [keyn])
+            send("c%d" % sl, [keyn])
         tag[0] = "r" + H
-        ts(64, T.fpad[:, a:a + 96:6], last(T.scw), 5.0, None, ALU.add, None, ["scw" + H], ["fpad" + H])
-        tt(96, c96(T.nb), c96(T.scb), K, ALU.not_equal, ["scb" + H, "k" + H], ["nb" + H], kb)
-        scan(c96(T.bc), T.keep[:], c96(T.fpad), ALU.mult, ALU.add, ["keep", "fpad" + H], ["bc" + H])
-        scan(T.s2[:, 2 * a:2 * a + 96], c96(T.nb), c96(sx), ALU.mult, ALU.max, ["nb" + H, sxn], ["s2b" + H])
-        tt(96, c96(T.nw), c96(T.bc), K, ALU.not_equal, ["bc" + H, "k" + H], ["nw" + H], kb)
-        tt(96, c96(T.ew), c96(T.bc), K, ALU.is_equal, ["bc" + H, "k" + H], ["ew" + H], kb)
-        scan(T.s2[:, 2 * a + 96:2 * a + 192], c96(T.nw), c96(sx), ALU.mult, ALU.max, ["nw" + H, sxn], ["s2w" + H])
-        tt(64, T.u1[:, 2 * z:2 * z + 32], T.s2[:, 2 * a + 5:2 * a + 192:6], T.coef[:], ALU.mult, ["s2b" + H, "s2w" + H, "coefa", "coefb"], ["u1" + H])
-        tt(64, c16(T.uu), T.u1[:, 2 * z:2 * z + 16], T.u1[:, 2 * z + 16:2 * z + 32], ALU.add, ["u1" + H], ["uu" + H])
-        ts(64, c16(T.tm), T.s2[:, 2 * a + 101:2 * a + 192:6], -20480.0, None, ALU.add, None, ["s2w" + H], ["tm" + H])
+        scan(96, c96(T.scw), T.dmin[:], K, ALU.add, ALU.min, ["dmin", kn], ["scw" + H], kb, arr)
+        if nd and not own and h == 0:
+            spread_dma(sl // 2, range(CFG["early"], 8), ["scw0"], CFG["td"][1])
+        tt(96, c96(T.nb), scb[:, so:so + 96], K, ALU.not_equal, ["scb" + H, kn], ["nb" + H], kb)
+        scan(96, back(bc, bo), back(T.drev, 0), back(T.scw, a), ALU.add, ALU.min, ["drev", "scw" + H], ["bc" + H], kb if own else [])
+        scan(96, c96(T.sb), c96(T.nb), sx, ALU.mult, ALU.max, ["nb" + H, "sx" + H], ["sb" + H], kb)
+        tt(96, ew, bc[:, bo:bo + 96], K, ALU.is_equal, ["bc" + H, kn], ["ew" + H], kb)
+        tt(96, c96(T.z), px, ew, ALU.mult, ["ew" + H, pxn], ["z" + H], kb)
+        scan(64, c96(T.st), T.keeph[:], c96(T.z), ALU.mult, ALU.add, ["keeph", "z" + H], ["st" + H])
+        if CFG["uuv"]:
+            ut, uo, tw, ub = T.uu, z, T.uu[:, 32 + z:48 + z], []
+            ts(64, T.uu[:, 64 + z:80 + z], last(T.st, a), 56.0, None, ALU.mult, None, ["st" + H], ["u1" + H])
+            ts(64, tw, last(T.st, a), 2048.0, None, ALU.add, None, ["st" + H], ["tw" + H])
+            tt(64, c16(T.uu), T.uu[:, 64 + z:80 + z], last(T.sb, a), ALU.add, ["u1" + H, "sb" + H], ["uu" + H])
+        else:
+            ut, uo, tw, ub = PK[h], 288, PK[h][:, 304:320], kb
+            mm(256, ut[:, uo:uo + 16], T.idf[:], last(T.sb, a), True, False, ["idf", "sb" + H], ["uu" + H], kb)
+            mm(64, ut[:, uo:uo + 16], T.i56[:], last(T.st, a), False, True, ["i56", "st" + H], ["uu" + H], kb)
+            mm(64, tw, T.idh[:], T.coffh[:, 96:112], True, False, ["idh", "coffh"], ["tw" + H], kb)
+            mm(64, tw, T.idh[:], last(T.st, a), False, True, ["idh", "st" + H], ["tw" + H], kb)
         tag[0] = "o" + H
         if own:
-            tt(64, T.tot[:, z:z + 14], T.uu[:, z:z + 14], T.key[:, 16 * slot + 2:16 * slot + 16], ALU.add, ["uu" + H, keyn], ["tot" + H])
-            tt(64, T.tot[:, z + 14:z + 16], T.uu[:, z + 14:z + 16], T.key[:, 16 * slot:16 * slot + 2], ALU.add, ["uu" + H, keyn], ["totb" + H])
+            tt(64, T.tot[:, z:z + 14], T.key[:, 16 * sl + 2:16 * sl + 16], ut[:, uo:uo + 14], ALU.add, ["uu" + H, keyn], ["tot" + H], ub)
+            tt(64, T.tot[:, z + 14:z + 16], T.key[:, 16 * sl:16 * sl + 2], ut[:, uo + 14:uo + 16], ALU.add, ["uu" + H, keyn], ["totb" + H], ub)
         else:
-            tt(64, c16(T.tot), c16(T.uu), T.cin[:, 16 * slot:16 * slot + 16], ALU.add, ["uu" + H], ["tot" + H, "totb" + H],
-               arr=("arc%d" % slot, "c%d" % slot, CFG["ring"]))
-        db, ed = PK[h][:, 256:352], PK[h][:, 384:480]
+            tt(64, c16(T.tot), T.cin[:, 16 * sl:16 * sl + 16], ut[:, uo:uo + 16], ALU.add, ["uu" + H], ["tot" + H, "totb" + H], ub,
+               arr=("arc%d" % sl, "c%d" % sl, CFG["ring"]))
         ts(64, c16(T.nwv), c16(T.tot), 3, 4095, ALU.arith_shift_right, ALU.bitwise_and, ["tot" + H, "totb" + H], ["nwv" + H])
-        tt(64, T.dpad[:, a:a + 96:6], c16(T.nwv), c16(T.tm), ALU.subtract, ["nwv" + H, "tm" + H], ["dpad" + H])
-        scan(db, T.keep[:], c96(T.dpad), ALU.mult, ALU.add, ["keep", "dpad" + H], ["db" + H], kb)
-        tt(96, ed, c96(T.ew), db, ALU.mult, ["ew" + H, "db" + H], ["ed" + H], kb)
-        tt(96, c96(T.px), c96(T.px), ed, ALU.add, ["px" + H, "ed" + H], ["px" + H], kb)
-        for n in range(8):
-            for jj in range(4):
-                place(lambda m: PK[h][32 * jj:32 * jj + m, 128 + n:224:8], n,
-                      lambda lo: T.px[:, a + 12 * (2 * jj + lo):a + 12 * (2 * jj + lo) + 12], ["px" + H], ["cv" + H], kb)
+        tt(64, T.dpad[:, a:a + 96:6], c16(T.nwv), tw, ALU.subtract, ["nwv" + H, "tw" + H], ["dpad" + H], ub)
+        scan(96, c96(T.db), T.keep[:], c96(T.dpad), ALU.mult, ALU.add, ["keep", "dpad" + H], ["db" + H])
+        tt(96, ew, c96(T.db), ew, ALU.mult, ["ew" + H, "db" + H], ["ew" + H], kb)
+        tt(96, px, px, ew, ALU.add, [pxn, "ew" + H], [pxn], kb)
         if own:
+            for n in range(8):
+                for jj in range(4):
+                    place(lambda m: PK[h][32 * jj:32 * jj + m, 416 + n:512:8], n,
+                          lambda lo: src[:, a + 12 * (2 * jj + lo):a + 12 * (2 * jj + lo) + 12], 12, [pxn], ["cv" + H], kb)
             for b in range(2):
-                ts(64, T.yo[:, :, 16 * h + 8 * b:16 * h + 8 * b + 8], PK[h][:, 128 + 48 * b:176 + 48 * b], 2048.0, None, ALU.add, None,
+                ts(64, T.yo[:, :, 16 * b + 8 * h:16 * b + 8 * h + 8], PK[h][:, 416 + 48 * b:464 + 48 * b], 2048.0, None, ALU.add, None,
                    ["cv" + H], ["yo%d" % (2 * h + b)], kb)
         else:
-            ts(96, c96(T.off), PK[h][:, 128:224], 2048.0, None, ALU.add, None, ["cv" + H], ["off%d" % (2 * h), "off%d" % (2 * h + 1)], kb)
-            tag[0] = "x" + H
-            tt(96, c96(T.sx), c96(T.sx), ed, ALU.add, ["sx" + H, "ed" + H], ["sx" + H], kb)
+            lists(h, sl < 4)
 
-    first_sources(0)
-    first_sources(1)
+    def give_back(h):
+        dma("y", "dsy%d" % h, T.sy[4 * h:4 * h + 4], T.vsb[:, 256 * h:256 * h + 256], r=vall[4 * h:4 * h + 4], w=["sy%d" % h])
+        if rank // 4 == h:
+            c = 32 * (rank % 4)
+            dma("y", "doy", T.ly[me], T.vsb[c:c + 32, 256 * h:256 * h + 256], r=vall[4 * h:4 * h + 4], w=["ly"])
+
     for t in range(RO):
-        for q in range(4):
-            for k in range(2):
-                gather(q, k, "v" if (q, k) in CFG["vg"][t] else "s", t % 2)
-        for q in range(4):
+        final = t == RO - 1
+        now[:] = [t, "L" if final else ""]
+        for i in range(8):
+            gather(i, t % 2)
+        if final:
+            send("s", ["px0", "px1"])
+            cp(64, T.sl[:, 2 * me:2 * me + 2, :], T.px[:, 24 * rank:24 * rank + 24], ["px0", "px1"], ["slo"])
+        for q in range(6):
             if q >= 2:
-                scores(q - 2)
-            sums(q, 0)
-            sums(q, 1)
-            clamp(q)
-        scores(2)
-        scores(3)
-        if t < RO - 1:
-            spread(0, (t + 1) % 2)
-            spread(1, (t + 1) % 2)
+                products(q - 2, final)
+            if final and q == 3:
+                send("y0", ["sy0"])
+            if q < 4:
+                sums(2 * q, t, nd and q < 2 and not final)
+                sums(2 * q + 1, t, nd and q < 2 and not final)
+            if final and q in (1, 3):
+                give_back(q // 2)
+        if not final:
+            spread(0, t)
+            spread(1, t)
             for h in range(2):
                 renew(h, 2 * t + h, False)
-            if t == RO - 2:
-                send("s0", ["sx0"])
-                send("s1", ["sx1"])
-    dma("y", "dsy", T.sy[:], T.vsb[:], r=vall, w=["sy"])
-    dma("y", "doy", T.ly[me], T.vsb[16 * rank:16 * rank + 16, :], r=vall, w=["ly"])
+    now[1] = "O"
+    send("y1", ["sy1"])
+    y = "y%d" % (rank // 4)
+    for k in range(2):
+        dma("y", "dya", T.ya[:, 256 * k:256 * k + 256], T.ly[:, 64 * k:64 * k + 64, :], r=["ly"], arr=("ar" + y, y, 5.0))
     for h in range(2):
-        a = 96 * h
-        tag[0] = "t%d" % h
-        cp(96, T.ks[:, a:a + 96], PK[h][:, 0:96], ["k%d" % h], ["ks%d" % h], ["pk%d" % h])
-        send("k%d" % h, ["ks%d" % h])
-        cp(64, T.kl[:, a + 12 * me:a + 12 * me + 12], T.ks[:, a + 12 * rank:a + 12 * rank + 12], ["ks%d" % h], ["kl%d" % h])
-        cp(64, T.sl[:, a + 12 * me:a + 12 * me + 12], T.sx[:, a + 12 * rank:a + 12 * rank + 12], ["sx%d" % h], ["slo%d" % h])
-    send("y", ["sy"])
-    dma("y", "dya", T.ya[:], T.ly[:], r=["ly"], arr=("ary", "y", 5.0))
-    for h in range(2):
-        a = 96 * h
-        tt(192, T.px[:, a:a + 96], T.sl[:, a:a + 96], T.coff[:], ALU.subtract, ["slo%d" % h] + coff, ["px%d" % h, "sl%d" % h],
-           arr=("ars%d" % h, "s%d" % h, 6.5))
-        cp(96, PK[h][:, 0:96], T.kl[:, a:a + 96], ["kl%d" % h], ["k%d" % h], ["pk%d" % h], arr=("ark%d" % h, "k%d" % h, 6.0))
+        tag[0] = "x%d" % h
+        cp(64, T.po[:, 96 * h:96 * h + 96], T.sl[:, :, 6 * h:6 * h + 6], ["slo"], ["po%d" % h], arr=("ars", "s", 6.5))
+        keyed(h, T.po, "po")
         renew(h, 6 + h, True)
     dma("s", "dys", T.ys[:], T.yo[:], r=["yo0", "yo1", "yo2", "yo3"])
-    emit(g, T, ops)
-    g.wait_ge(T.sem.sent, got[(core, "sent")])
+    return ops

from concourse.bass import DstId, RemoteDMATransfer
from concourse.mybir import AluOpType as ALU, ActivationFunctionType as ACT

N, U, D, RO, W = 8, 512, 6, 4, 4096
BIG = float(2 ** 26)
CFG = {"cyc": 0.00086, "gc": 1.56, "pe": 0.00046, "hop": 0.2, "lag0": 0.05, "ring": 2.2, "second": {}, "least": 0.1, "vspread": [], "vfirst": [0, 2, 4, 6],
       "ta": [3.0, 5.6], "tw": 5.6, "tp": 5.0, "tk": 4.0, "nd": 8, "td": [3.0, 3.6], "early": 3, "uuv": 0, "twice": [], "xbank": [0, 1, 0, 1],
       "aclamp": [], "fine": 0, "fused": [0, 4], "tries": 3000,
       "tails": {"k2": 11.0, "k3": 9.5, "y1": 7.0}}

SCRATCH = {
    "sa": ("dram", [8, 128, 64], "bfloat16"), "sw": ("dram", [8, 128, 28], "int32"), "sy": ("dram", [8, 128, 64], "bfloat16"),
    "lw": ("dram", [8, 128, 28], "int32"), "ly": ("dram", [8, 128, 64], "bfloat16"),
    "ra": ("dram", [2, 128, 64], "bfloat16"), "rw": ("dram", [2, 128, 28], "int32"), "ry": ("dram", [2, 128, 64], "bfloat16"),
    "rk": ("sbuf", [128, 4 * 12], "float32"), "rc": ("sbuf", [128, 6 * 16], "float32"),
    "rp": ("sbuf", [128, 48], "float16"), "rs": ("sbuf", [128, 48], "float16"),
    "ja": ("sbuf", [128, 128], "bfloat16"), "jb": ("sbuf", [128, 8], "bfloat16"), "jd": ("sbuf", [128, 128], "bfloat16"),
    "jw": ("sbuf", [128, 128], "bfloat16"), "jv": ("sbuf", [128, 128], "bfloat16"), "jp": ("sbuf", [128, 128], "bfloat16"),
    "jq": ("sbuf", [128, 128], "bfloat16"), "jr": ("sbuf", [128, 128], "bfloat16"),
    "top": ("sbuf", [128, 1], "float32"), "b8": ("sbuf", [128, 24], "float32"), "jz": ("sbuf", [128, 256], "bfloat16"),
    "idf": ("sbuf", [128, 128], "float32"), "idh": ("sbuf", [128, 128], "float16"), "idb": ("sbuf", [128, 128], "bfloat16"),
    "i104": ("sbuf", [128, 128], "float16"), "i56": ("sbuf", [128, 128], "float16"),
    "turn": ("sbuf", [128, 128], "float16"), "unturn": ("sbuf", [128, 128], "bfloat16"),
    "sel": ("sbuf", [128, 15 * 128], "float16"), "rep": ("sbuf", [128, 16 * 128], "bfloat16"), "zz": ("sbuf", [128, 256], "float16"),
    "dmax": ("sbuf", [128, 96], "float32"), "dmin": ("sbuf", [128, 96], "float32"), "drev": ("sbuf", [128, 96], "float32"),
    "keep": ("sbuf", [128, 96], "float32"), "keeph": ("sbuf", [128, 96], "float16"),
    "coff": ("sbuf", [128, 112], "float32"), "coffh": ("sbuf", [128, 112], "float16"),
    "ysr": ("sbuf", [128, 6, 32], "int32"), "py": ("sbuf", [128, 192], "float16"), "pq": ("sbuf", [128, 192], "float16"),
    "wi": ("sbuf", [128, 256], "int32"), "wq": ("sbuf", [128, 256], "float16"), "va": ("sbuf", [128, 512], "bfloat16"),
    "win": ("sbuf", [128, 2 * 4096], "bfloat16"), "off": ("sbuf", [128, 192], "uint16"), "vsb": ("sbuf", [128, 512], "bfloat16"),
    "p": ("sbuf", [128, 3072], "bfloat16"), "pw": ("sbuf", [128, 3072], "float16"), "pv": ("sbuf", [128, 3072], "float32"),
    "px": ("sbuf", [128, 192], "float16"), "wk": ("sbuf", [128, 1536], "bfloat16"),
    "scb": ("sbuf", [128, 192], "float32"), "scw": ("sbuf", [128, 192], "float32"), "nb": ("sbuf", [128, 192], "float32"),
    "bc": ("sbuf", [128, 192], "float32"), "sb": ("sbuf", [128, 192], "float32"), "z": ("sbuf", [128, 192], "float16"),
    "st": ("sbuf", [128, 192], "float16"), "dpad": ("sbuf", [128, 192], "float32"), "db": ("sbuf", [128, 192], "float32"),
    "uu": ("sbuf", [128, 96], "float32"), "tot": ("sbuf", [128, 32], "int32"), "nwv": ("sbuf", [128, 32], "int32"),
    "key": ("sbuf", [128, 8 * 16], "float32"), "cin": ("sbuf", [128, 6 * 16], "float32"),
    "sl": ("sbuf", [128, 16, 12], "float16"), "po": ("sbuf", [128, 192], "float16"),
    "ks": ("sbuf", [128, 192], "float32"), "kl": ("sbuf", [128, 192], "float32"), "yo": ("sbuf", [128, 6, 32], "float32"),
    "pw0": ("psum", [128, 512], "float32"), "pw1": ("psum", [128, 512], "float32"),
    "pe0": ("psum", [128, 512], "float32"), "pe1": ("psum", [128, 512], "float32"),
    "ps0": ("psum", [128, 512], "float32"), "ps1": ("psum", [128, 512], "float32"),
    "pk0": ("psum", [128, 512], "float32"), "pk1": ("psum", [128, 512], "float32"),
}
PHASES = ["w", "a", "p", "c0", "c1", "c2", "c3", "c4", "c5", "s", "k0", "k1", "y0", "k2", "k3", "y1"]
SEMAPHORES = (["cv", "cs", "ct", "cg", "sent", "dsa", "dsw", "dsr", "doa", "dow", "dlw", "dw0", "dw1", "dw2",
               "dsy0", "dsy1", "doy", "dya", "dys", "ara0", "ara1"]
              + ["ar" + p for p in PHASES if p != "a"] + ["rl" + p for p in PHASES])
_PLAN = {}


def slot(r):
    return 2 * (r % 4) + r // 4


def _bits(engines):
    return sum(1 << e for e in engines)


def _perms(xs):
    if len(xs) <= 1:
        yield list(xs)
        return
    for i in range(len(xs)):
        for r in _perms(xs[:i] + xs[i + 1:]):
            yield [xs[i]] + r


def make_plan(T, topo):
    cores = list(T.cores)
    same = lambda a, b: a in topo.cores_of(b)
    cost = lambda a, b: 1 if same(a, b) else (3 if topo.may_write(a, b) else 10)
    best = None
    for pm in _perms(list(range(1, N))):
        ring = [0] + pm
        c = sum(cost(cores[ring[(k + 1) % N]], cores[ring[k]]) for k in range(N))
        if best is None or c < best[0]:
            best = (c, ring)
    ring = best[1]
    net = [ring.index(r) for r in range(N)]
    calls, got, order = {}, {}, []

    def add(src, ph, transfers):
        if transfers:
            calls.setdefault(src, {}).setdefault(ph, []).append(transfers)
        for dst, mask, sem, a, b in transfers:
            got[(dst, sem)] = got.get((dst, sem), 0) + bin(mask).count("1")
            got[(src, "sent")] = got.get((src, "sent"), 0) + bin(mask).count("1")

    used = set()
    for r in range(N):
        c = cores[r]
        sib = [d for d in range(N) if d != r and same(cores[d], c)]
        far = [d for d in range(N) if not same(cores[d], c) and topo.may_write(c, cores[d])]
        oth = [d for d in range(N) if not topo.may_write(c, cores[d]) and d != r]
        pairs = []
        for d in oth:
            if pairs and same(cores[pairs[-1][0]], cores[d]):
                pairs[-1].append(d)
            else:
                pairs.append([d])
        relay = []
        for pr in pairs:
            assert len(pr) == 2 and pr[1] == pr[0] + 1
            cand = [x for x in topo.cores_of(c) if x not in cores and x not in used and topo.may_write(x, cores[pr[0]])]
            cand.sort(key=lambda x: topo.die(x) != topo.die(c))
            relay.append(cand[0])
            used.add(cand[0])
        assert len(sib) == 1 and len(far) == 2 and len(pairs) == 2
        on = topo.engines(c, cores[sib[0]])
        off = topo.engines(c, cores[far[0]])
        loc = [e for e in on if e not in off]

        def dram_phase(ph, ar, sname, lname, rname, sslot, lslot, k, to):
            add(c, ph, [(relay[a], _bits(loc[4 * a + 2 * b:4 * a + 2 * b + k]), "rl" + ph, (sname, sslot(pairs[a][b])), (rname, b))
                        for a in range(2) for b in range(2) if pairs[a][0] in to])
            add(c, ph, [(cores[d], _bits(off[2 * b:2 * b + k]), ar, (sname, sslot(d)), (lname, lslot)) for b, d in enumerate(far + sib) if d in to])
            for a in range(2):
                ro = topo.engines(relay[a], cores[pairs[a][0]])
                pick = [ro[0:1], ro[4:5]] if k == 1 else [ro[0:4], ro[4:8]]
                if pairs[a][0] in to:
                    add(relay[a], ph, [(cores[pairs[a][b]], _bits(pick[b]), ar, (rname, b), (lname, lslot)) for b in range(2)])

        def sbuf_phase(ph, sname, at, rname, ro_, land, n, to):
            add(c, ph, [(relay[a], _bits(on[8 * a:8 * a + 8]), "rl" + ph, (sname, at(pairs[a][0]), 2 * n), (rname, ro_, 2 * n))
                        for a in range(2) if pairs[a][0] in to])
            add(c, ph, [(cores[d], _bits(off[4 * b:4 * b + 4] if b < 2 else loc), "ar" + ph, (sname, at(d), n), land)
                        for b, d in enumerate(far + sib) if d in to])
            for a in range(2):
                ro = topo.engines(relay[a], cores[pairs[a][0]])
                if pairs[a][0] in to:
                    add(relay[a], ph, [(cores[pairs[a][b]], _bits(ro[4 * b:4 * b + 4]), "ar" + ph, (rname, ro_ + n * b, n), land) for b in range(2)])

        def half_phase(ph, sname, at, rname, ro_, land, n, to):
            pair = [d for pr in pairs for d in pr if d in to]
            add(c, ph, [(relay[b], _bits(on[8 * b:8 * b + 8]), "rl" + ph, (sname, at(d), n), (rname, ro_, n)) for b, d in enumerate(pair)])
            add(c, ph, [(cores[d], _bits(off[4 * b:4 * b + 4] if b < 2 else on), "ar" + ph, (sname, at(d), n), land)
                        for b, d in enumerate(far + sib) if d in to])
            for b, d in enumerate(pair):
                add(relay[b], ph, [(cores[d], topo.mask(relay[b], cores[d]), "ar" + ph, (rname, ro_, n), land)])

        every = range(N)
        order.append(pairs[0] + pairs[1] + far + sib + [r])
        dram_phase("w", "arw", "sw", "lw", "rw", lambda d: net[d], r, 1, every)
        land = ("va", 64 * r, 64)
        add(c, "a", [(relay[a], _bits(loc[4 * a + 2 * b + 1:4 * a + 2 * b + 2]), "rla", ("sa", net[pairs[a][b]]), ("ra", b))
                     for a in range(2) for b in range(2)])
        add(c, "a", [(cores[d], _bits(e), "ara0", ("sa", net[d]), land) for d, e in zip(far + sib, (off[1:4:2], off[5:8:2], loc[0:3:2]))])
        for a in range(2):
            ro = topo.engines(relay[a], cores[pairs[a][0]])
            add(relay[a], "a", [(cores[pairs[a][b]], _bits(ro[4 * b:4 * b + 4]), "ara1", ("ra", b), land) for b in range(2)])
        sbuf_phase("p", "pq", lambda d: 24 * order[r].index(d), "rp", 0, ("px", 24 * r, 24), 24, every)
        sbuf_phase("s", "px", lambda d: 24 * d, "rs", 0, ("sl", 2 * net[r], 2), 24, every)
        for h in range(2):
            half = range(4 * h, 4 * h + 4)
            dram_phase("y%d" % h, "ary%d" % h, "sy", "ly", "ry", lambda d: d, net[r], 2, half)
            for b in range(2):
                n = 2 * h + b
                half_phase("k%d" % n, "ks", lambda d: 48 * n + 12 * (d % 4), "rk", 12 * n, ("kl", 96 * b + 12 * net[r], 12), 12, half)
        d = ring[(net[r] - 1) % N]
        for n in range(6):
            ph = "c%d" % n
            if topo.may_write(c, cores[d]):
                add(c, ph, [(cores[d], topo.mask(c, cores[d]), "ar" + ph, ("key", 16 * n, 16), ("cin", 16 * n, 16))])
            else:
                x = relay[0] if d in pairs[0] else relay[1]
                add(c, ph, [(x, topo.mask(c, x), "rl" + ph, ("key", 16 * n, 16), ("rc", 16 * n, 16))])
                add(x, ph, [(cores[d], topo.mask(x, cores[d]), "ar" + ph, ("rc", 16 * n, 16), ("cin", 16 * n, 16))])
    return {"net": net, "order": order, "calls": calls, "got": got}


def _side(T, s):
    return T[s[0]][s[1]] if len(s) == 2 else T[s[0]][:, s[1]:s[1] + s[2]]


def remote(g, core, T, topo, transfers):
    tr = []
    for dst, mask, sem, a, b in transfers:
        rid, pid = topo.addr(dst, core)
        tr.append(RemoteDMATransfer(dst_ids=[DstId(rid=rid, pnc=pid)], dma_engine_mask=mask, remote_sem=T.sem[sem],
                                    src=_side(T, a), dst=_side(T, b)))
    g.remote_dma_fused(tr, local_sem=T.sem.sent)


def arrange(ops):
    lastw, readers, banks, chain, sent = {}, {}, {}, {}, {}
    for i, o in enumerate(ops):
        deps, order = set(), {}
        for x in o["r"]:
            deps.update(lastw.get(x, []))
        for x in o["w"]:
            deps.update(lastw.get(x, []))
            deps.update(readers.get(x, []))
        for b in o["b"]:
            deps.update(k for e, k in banks.get(b, {}).items() if e != o["e"])
            if o["e"] in banks.get(b, {}):
                order[banks[b][o["e"]]] = 0.0
        if o["e"] in "gy" or o["dma"]:
            if o["e"] in chain:
                order[chain[o["e"]]] = 0.0
            chain[o["e"]] = i
        deps.discard(i)
        hard = set()
        for k in deps:
            d = ops[k]
            if (o["e"] == "t" and d["e"] == "t") or (o["dma"] and d["dma"] == o["dma"]) or d["rem"]:
                order[k] = 0.0
            else:
                hard.add(k)
                d["need"] = True
                order[k] = d["lag"] if d["dma"] else (CFG["lag0"] if d["e"] == o["e"] else CFG["hop"])
        if o["after"]:
            order[sent[o["after"][0]]] = o["after"][1]
        if o["rem"] and o["rem"] not in sent:
            sent[o["rem"]] = i
        o["deps"], o["order"], o["succ"] = hard, order, []
        for k in order:
            ops[k]["succ"].append(i)
        for x in o["r"]:
            readers.setdefault(x, []).append(i)
        for x in o["w"]:
            lastw[x] = [i]
            readers[x] = []
        for b in o["b"]:
            banks.setdefault(b, {})[o["e"]] = i
    return in_order(ops)


def place_all(ops, pre, key, back):
    n = len(ops)
    key = list(key)
    for i in (range(n - 1, -1, -1) if back else range(n)):
        for k, lag in pre[i]:
            if key[k] >= key[i]:
                key[i] = key[k] + 1e-6
    starts, ends = {e: [] for e in "vstgy"}, {e: [] for e in "vstgy"}
    fin = [0.0] * n
    for i in sorted(range(n), key=lambda x: key[x]):
        t = 0.0
        for k, lag in pre[i]:
            if fin[k] + lag > t:
                t = fin[k] + lag
        e, c = ops[i]
        st, en = starts[e], ends[e]
        j = m = len(st)
        while j and en[j - 1] > t + 1e-9:
            j -= 1
        while j < m and st[j] < t + c - 1e-9:
            if en[j] > t:
                t = en[j]
            j += 1
        st.insert(j, t)
        en.insert(j, t + c)
        fin[i] = t + c
    return fin


def in_order(ops):
    n = len(ops)
    ec = [(o["e"], o["c"]) for o in ops]
    tail = [o["tail"] for o in ops]
    pre = [list(o["order"].items()) for o in ops]
    post = [[] for o in ops]
    seen, names = {}, []
    for i, o in enumerate(ops):
        name = (o["round"], o["tag"], o["e"])
        seen[name] = seen.get(name, -1) + 1
        names.append((name, seen[name]))
        for k, lag in pre[i]:
            post[k].append((i, lag))
    state = [12345]

    def rnd():
        state[0] = (state[0] * 1103515245 + 12345) % 2147483648
        return state[0] / 2147483648.0

    def both(key):
        one = place_all(ec, pre, key, False)
        two = place_all(ec, pre, [-f for f in place_all(ec, post, [-f - t for f, t in zip(one, tail)], True)], False)
        return min([(max(f + t for f, t in zip(fin, tail)), k, fin) for k, fin in enumerate((one, two))])

    kind = "order"
    if kind in _PLAN:
        best = both([_PLAN[kind].get(x, 0.0) for x in names])
    else:
        key = [0.0] * n
        for i in range(n - 1, -1, -1):
            key[i] = min([key[k] - lag for k, lag in post[i]] + [-tail[i]]) - ec[i][1]
        best = both(key)
        for _ in range(CFG["tries"]):
            lo, wide, size, whole = best[0] * rnd(), (2.0, 6.0, 12.0)[int(3 * rnd())], (0.2, 0.5, 1.5)[int(3 * rnd())], rnd() < 0.5
            shift, key = {}, []
            for i in range(n):
                x = best[2][i] - ec[i][1]
                if lo < x < lo + wide:
                    if not whole:
                        x += size * (rnd() - rnd())
                    else:
                        if names[i][0] not in shift:
                            shift[names[i][0]] = 2 * size * (rnd() - rnd()) if rnd() < 0.3 else 0.0
                        x += shift[names[i][0]]
                key.append(x)
            new = both(key)
            if new[0] <= best[0]:
                best = new
        _PLAN[kind] = {names[i]: best[2][i] - ec[i][1] for i in range(n)}
    return sorted(range(n), key=lambda i: (round(best[2][i] - ec[i][1], 7), i))


def emit(g, T, ops):
    queue = {"v": g.vector, "s": g.scalar, "t": g.tensor, "g": g, "y": g.sync}
    counter = {"v": "cv", "s": "cs", "t": "ct", "g": "cg"}
    ndma, count, known = {}, {}, {}
    for o in ops:
        if o["dma"]:
            ndma[o["dma"]] = ndma.get(o["dma"], 0) + 1
    for i in arrange(ops):
        o = ops[i]
        q = queue[o["e"]]
        want = {}
        for k in o["deps"]:
            d = ops[k]
            s, val = (d["dma"], 16 * ndma[d["dma"]]) if d["dma"] else (counter[d["e"]], d["n"])
            want[s] = max(want.get(s, 0), val)
        for s, val in o["wait"]:
            want[s] = max(want.get(s, 0), val)
        for s, val in want.items():
            if known.get((o["e"], s), 0) < val:
                q.wait_ge(T.sem[s], val)
                known[(o["e"], s)] = val
        ins = o["f"](q)
        if o["dma"]:
            ins.then_inc(T.sem[o["dma"]], 16)
        elif o.get("need"):
            count[o["e"]] = count.get(o["e"], 0) + 1
            o["n"] = count[o["e"]]
            ins.then_inc(T.sem[counter[o["e"]]], 1)
    for e, n in count.items():
        g.wait_ge(T.sem[counter[e]], n)
    for s, n in ndma.items():
        g.sync.wait_ge(T.sem[s], 16 * n)


def rank_program(g, core, T, topo):
    if "p" not in _PLAN:
        _PLAN["p"] = make_plan(T, topo)
    plan = _PLAN["p"]
    calls, got = plan["calls"].get(core), plan["got"]
    rank = T.rank_of(core)
    if calls is None:
        return
    if rank is None:
        for ph in PHASES:
            if ph in calls:
                g.wait_ge(T.sem["rl" + ph], got[(core, "rl" + ph)])
                for tr in calls[ph]:
                    remote(g, core, T, topo, tr)
    else:
        if "order" not in _PLAN:
            arrange(rank_calls(g, T.cores[N - 1], N - 1, T, topo, plan))
        emit(g, T, rank_calls(g, core, rank, T, topo, plan))
    g.wait_ge(T.sem.sent, got[(core, "sent")])


def rank_calls(g, core, rank, T, topo, plan):
    calls, got = plan["calls"][core], plan["got"]
    me = plan["net"][rank]
    ops = []
    tag, now = ["h"], [-1, "A"]
    cyc, pe, nd = CFG["cyc"], CFG["pe"], CFG["nd"]

    def op(e, f, c, r=(), w=(), b=(), arr=None, dma=None, rem=None, lag=2.2):
        wait = [(arr[0], got[(core, arr[0])])] if arr else []
        c = max(c, CFG["least"]) if e in "vs" and not dma else c
        ops.append({"e": e, "f": f, "c": c, "r": list(r), "w": list(w), "b": list(b), "wait": wait,
                    "after": arr[1:] if arr else None, "dma": dma, "rem": rem, "tag": now[1] + tag[0], "round": now[0], "lag": lag,
                    "tail": lag if dma else CFG["tails"].get(rem, 0.0)})

    def send(ph, reads):
        for tr in calls[ph]:
            op("g", lambda q, tr=tr: remote(g, core, T, topo, tr), 0.3, r=reads, rem=ph)

    def dma(e, sem, out, in_, r=(), w=(), arr=None, lag=2.2):
        op(e, lambda q: q.dma_start(out, in_), 0.05, r=r, w=w, arr=arr, dma=sem, lag=lag)

    def ts(n, out, in0, s1, s2, o0, o1, r, w, b=()):
        if o1 is None:
            op("v", lambda q: q.tensor_scalar(out, in0, s1, None, o0), n * cyc, r, w, b)
        else:
            op("v", lambda q: q.tensor_scalar(out, in0, s1, s2, o0, o1), n * cyc, r, w, b)

    def tt(n, out, in0, in1, o, r, w, b=(), arr=None):
        op("v", lambda q: q.tensor_tensor(out, in0, in1, o), n * cyc, r, w, b, arr)

    def cp(n, out, in_, r, w, b=(), arr=None):
        op("v", lambda q: q.tensor_copy(out, in_), n * cyc, r, w, b, arr)

    def scan(n, out, d0, d1, o0, o1, r, w, b=(), arr=None):
        op("v", lambda q: q.tensor_tensor_scan(out, d0, d1, 0.0, o0, o1), n * cyc, r, w, b, arr)

    def fill(n, ap, val, w):
        op("v", lambda q: q.memset(ap, val), n * cyc, (), w)

    def mm(n, out, lhsT, rhs, start, stop, r, w, b, arr=None):
        op("t", lambda q: q.matmul(out, lhsT, rhs, start, stop), n * pe, r, w, b, arr)

    def act(n, out, in_, r, w, b=()):
        op("s", lambda q: q.activation(out, in_, ACT.Copy), n * cyc, r, w, b)

    def iota(name, ap, pattern, base=0):
        op("g", lambda q: q.iota(ap, pattern, base, -1, allow_small_or_imprecise_dtypes=True), 0.4, w=[name])

    def pick(out, name, val, w, scale=None):
        n = out.shape[1]
        ts(64, out, T[name][:, 0:n], float(val), scale, ALU.is_equal, ALU.mult if scale else None, [name], w)

    PW, PE, PK = [T.pw0, T.pw1], [T.pe0, T.pe1], [T.pk0, T.pk1]
    XB = [(T.ps0, "ps0"), (T.ps1, "ps1"), (T.pe0, "pe0"), (T.pe1, "pe1")]
    block = lambda t, k: t[:, 128 * k:128 * k + 128]

    dma("s", "dsw", T.sw[:, 0:109, :], T.wt[:, 0:3052], w=["sw0"])
    dma("y", "dsw", T.sw[:, 110:128, :], T.bs[:, 8:512], w=["sw1"])
    dma("s", "dsw", T.sw[:, 109, 0:20], T.wt[:, 3052:3072], w=["sw2"])
    dma("y", "dsw", T.sw[:, 109, 20:28], T.bs[:, 0:8], w=["sw3"])
    dma("s", "dsr", T.ysr[:], T.sr[:], w=["ysr"])
    dma("y", "dsa", T.sa[:], T.a0[:], w=["sa"])
    dma("y", "doa", T.va[:, 64 * rank:64 * rank + 64], T.a0[16 * me:16 * me + 16, :], w=["va"])
    op("y", lambda q: q.dma_start(T.lw[rank], T.sw[me]), 0.05, ["sw0", "sw1", "sw2", "sw3"], ["lw"], dma="dow")
    iota("jz", T.jz[:], [[16, 8], [-200, 2], [1, 16]], 200)
    iota("jr", T.jr[:], [[0, 8], [8, 16]])
    iota("jd", T.jd[:], [[1, 128]])
    iota("jb", T.jb[:], [[16, 8]])
    send("w", ["sw0", "sw1", "sw2", "sw3"])
    send("a", ["sa"])
    dma("y", "dlw", T.wi[0:112, :], T.lw[:], r=["lw"], w=["wi"], arr=("arw", "w", CFG["tw"]))
    ts(128, T.zz[:], T.jz[:], 0.0, None, ALU.is_equal, None, ["jz"], ["zz"])

    def place(out, a, rhs, n, r, w, b, arr=None):
        mm(32, out(32), T.zz[:, 32 * a:32 * a + 32], rhs(1), True, False, r + ["zz"], w, b, arr)
        mm(max(16, n), out(16), T.zz[:, 32 * a + 16:32 * a + 32], rhs(0), False, True, r + ["zz"], w, b)

    tag[0] = "i"
    for q in range(4):
        ts(64, T.py[:, 48 * q:48 * q + 48], T.ysr[:, :, 8 * q:8 * q + 8], -2048.0, None, ALU.add, None, ["ysr"], ["py%d" % q])
    order = plan["order"][rank]
    for k in range(2):
        for c, d in enumerate(order[4 * k:4 * k + 4]):
            for n in range(4):
                place(lambda m: PK[k][32 * n:32 * n + m, 24 * c:24 * c + 24], plan["net"][d],
                      lambda lo: T.py[:, 2 * n + lo::8], 24, ["py%d" % q for q in range(4)], ["cv%d" % k], ["pk%d" % k])
        cp(96, T.pq[:, 96 * k:96 * k + 96], PK[k][:, 0:96], ["cv%d" % k], ["pq%d" % k], ["pk%d" % k])
        op("g", lambda q, k=k: remote(g, core, T, topo, calls["p"][k]), 0.3, r=["pq%d" % k], rem="p")
    cp(64, T.px[:, 24 * rank:24 * rank + 24], T.pq[:, 168:192], ["pq1"], ["px0", "px1"])
    iota("jw", T.jw[:], [[14, 4], [1, 2], [0, 16]])
    iota("ja", T.ja[:], [[0, 8], [1, 16]])
    for c in range(8):
        pick(block(T.rep, 8 + c), "jr", -c, ["rep%d" % (8 + c)])

    tag[0] = "h"
    for j in range(8):
        pick(block(T.rep, j), "ja", -16 * j, ["rep%d" % j])
    for name, scale in (("idh", None), ("idb", None), ("i104", 104.0)) + (() if CFG["uuv"] else (("idf", None), ("i56", 56.0))):
        pick(T[name][:], "jd", 0, [name], scale)
    for h in range(2):
        for s in range(D + 1):
            pick(block(T.sel, 7 * h + s), "jw", -56 * h - 2 * s, ["sel%d" % (7 * h + s)])
    ts(64, T.b8[:, 8:16], T.jb[:], -16.0, None, ALU.is_gt, None, ["jb"], ["b8a"])
    ts(64, T.b8[:, 16:24], T.jb[:], 0.0, 8.0, ALU.is_le, ALU.mult, ["jb"], ["b8b"])
    tt(64, T.b8[:, 0:8], T.b8[:, 8:16], T.b8[:, 16:24], ALU.mult, ["b8a", "b8b"], ["b8"])
    if nd:
        iota("jp", T.jp[:], [[1, 16], [16, 8]])
        iota("jq", T.jq[:], [[1, 8], [8, 16]])
        iota("jv", T.jv[:], [[0, 16], [14, 4], [1, 2]])
        pick(T.turn[:], "jp", 0, ["turn"])
        pick(T.unturn[:], "jq", 0, ["unturn"])
        pick(block(T.sel, 14), "jv", -12, ["sel14"])
    for name, val, first, at in (("dmax", 1.0, -BIG, 0), ("dmin", -1.0, BIG, 0), ("drev", 1.0, BIG, 5), ("keep", 1.0, 0.0, 0)):
        fill(96, T[name][:], val, [name])
        fill(64, T[name][:, at::6], first, [name])
    cp(96, T.keeph[:], T.keep[:], ["keep"], ["keeph"])
    fill(192, T.dpad[:], 0.0, ["dpad0", "dpad1"])
    fill(64, T.top[:], 255.0, ["top"])
    for s in range(D):
        fill(64, T.coff[:, s:96:6], float(4096 * (6 - s)), ["coff%d" % s])
    fill(64, T.coff[:, 96:112], 2048.0, ["coff6"])
    cp(112, T.coffh[:], T.coff[:], ["coff%d" % s for s in range(D + 1)], ["coffh"])

    part = lambda u, h, jj: ["win%d_%d_%d_%d" % (u, h, j, b) for j in (2 * jj, 2 * jj + 1) for b in range(4)]
    bydma = lambda u: ["wd%d_%d" % (u, j) for j in range(8)]
    winall = lambda u: [x for h in range(2) for jj in range(4) for x in part(u, h, jj)] + bydma(u)
    vall = ["v%d" % i for i in range(8)]

    tag[0] = "f"
    for n, r in enumerate(order[::-1]):
        ps, bank = XB[n % 4]
        for c in range(8):
            mm(64, ps[:, 64 * c:64 * c + 64], block(T.rep, 8 + c), T.va[:, 64 * r:64 * r + 64], True, True,
               ["rep%d" % (8 + c), "va"], [bank], [bank], ("ara%d" % (n // 4), "a", CFG["ta"][n // 4]))
        (cp if n in CFG["vfirst"] else act)(512, T.win[:, 512 * r:512 * r + 512], ps[:], [bank], part(0, r // 4, r % 4), [bank])
    tag[0] = "w"
    ts(256, T.wq[0:112, :], T.wi[0:112, :], 0.0, None, ALU.add, None, ["wi"], ["wq"])

    def keyed(h, px, name):
        H = str(h)
        tag[0] = "x" + H
        mm(96, PK[h][:, 192:288], T.i104[:], px[:, 96 * h:96 * h + 96], True, False, ["i104", name + H], ["sx" + H], ["pk" + H])
        mm(96, PK[h][:, 192:288], T.i104[:], T.coffh[:, 0:96], False, True, ["i104", "coffh"], ["sx" + H], ["pk" + H])

    def lists(h, more=True, arr=None):
        H = str(h)
        a = 96 * h
        tag[0] = "l" + H
        for n in range(8):
            for jj in range(4):
                place(lambda m: PK[h][32 * jj:32 * jj + m, 416 + n:512:8], n,
                      lambda lo: T.px[:, a + 12 * (2 * jj + lo):a + 12 * (2 * jj + lo) + 12], 12, ["px" + H], ["cv" + H], ["pk" + H], arr)
        ts(96, T.off[:, a:a + 96], PK[h][:, 416:512], 2048.0, None, ALU.add, None, ["cv" + H], ["off" + H], ["pk" + H])
        if more:
            keyed(h, T.px, "px")

    for h in range(2):
        lists(h, True, ("arp", "p", CFG["tp"]))

    def sources(i, u):
        return T.win[:, W * u:W * u + W].indirect(T.off[:, 24 * i:24 * i + 24])

    def gather(i, u):
        tag[0] = "g%d" % i
        op("s", lambda e: e.activation(T.p[:, 384 * i:384 * i + 384], sources(i, u), ACT.Copy), 0.06 + 384 * CFG["gc"] * cyc,
           winall(u) + ["off%d" % (i // 4)], ["p%d" % i])

    def sums(i, t, turned):
        k, I, a, h = i % 2, str(i), 384 * i, i // 4
        tag[0] = "w" + I
        ps, bank = XB[CFG["xbank"][i]]
        wb, xb, out = ["pw%d" % k], [bank], ps[:, 0:64]
        wq = T.wq[0:112, 64 * (i % 4):64 * (i % 4) + 64]
        sel = lambda c: T.sel[0:112, 128 * c:128 * c + 128]
        fused = i in CFG["fused"]
        kept = T.wk[:, 384 * h:384 * h + 384]
        if t == 0 or not fused:
            for s in range(D):
                mm(64, PW[k][:, 64 * s:64 * s + 64], sel(7 * h + s), wq, True, True, ["wq", "sel%d" % (7 * h + s)], wb, wb)
        tag[0] = "m" + I
        if fused and t > 0:
            op("v", lambda q: q.tensor_tensor(T.pw[:, a:a + 384], sources(i, t % 2), kept, ALU.mult), 0.05 + 384 * CFG["gc"] * cyc,
               winall(t % 2) + ["off%d" % (2 * h + k), "wk" + I], ["m" + I])
        else:
            tt(384, T.pw[:, a:a + 384], T.p[:, a:a + 384], PW[k][:, 0:384], ALU.mult, ["p" + I] + wb, ["m" + I], wb)
        if fused and t == 0:
            tag[0] = "k" + I
            act(384, kept, PW[k][:, 0:384], wb, ["wk" + I], wb)
            tag[0] = "m" + I
        c, there, back = (14, "turn", "unturn") if turned else (7 * h + 6, "idh", "idb")
        if i in CFG["second"]:
            mm(64, out, sel(7 * h + 6), wq, True, False, ["wq", "sel%d" % (7 * h + 6)], xb, xb)
            for s in range(D):
                mm(64, out, T.idh[:], T.pw[:, a + 64 * s:a + 64 * s + 64], False, s == 5, ["idh", "m" + I], xb, xb)
            tag[0] = "n" + I
            ts(64, out, out, 0.0, 255.0, ALU.max, ALU.min, xb, xb, xb)
            tag[0] = "a" + I
            ps, bank = XB[CFG["second"][i]]
            xb, two = [bank], ps[:, 0:64]
            mm(64, two, sel(c), wq, True, False, ["wq", "sel%d" % c], xb, xb)
            for s in range(D):
                mm(64, two, T[there][:], T.pw[:, a + 64 * s:a + 64 * s + 64], False, s == 5, [there, "m" + I], xb, xb)
            op("s", lambda q: q.activation(two, two, ACT.Relu, T.top[:], -1.0), 64 * cyc, xb + ["top"], xb, xb)
            op("s", lambda q: q.activation(T.vsb[:, 64 * i:64 * i + 64], two, ACT.Relu, T.top[:], -1.0), 64 * cyc, xb + ["top"], ["v" + I], xb)
            return
        mm(64, out, sel(c), wq, True, False, ["wq", "sel%d" % c], xb, xb)
        for s in range(D):
            mm(64, out, T[there][:], T.pw[:, a + 64 * s:a + 64 * s + 64], False, s == 5, [there, "m" + I], xb, xb)
        tag[0] = "n" + I
        if i in CFG["aclamp"]:
            op("s", lambda q: q.activation(out, out, ACT.Relu, T.top[:], -1.0), 64 * cyc, xb + ["top"], xb, xb)
            op("s", lambda q: q.activation(T.vsb[:, 64 * i:64 * i + 64], out, ACT.Relu, T.top[:], -1.0), 64 * cyc, xb + ["top"], ["v" + I], xb)
        else:
            ts(64, T.vsb[:, 64 * i:64 * i + 64], out, 0.0, 255.0, ALU.max, ALU.min, xb, ["v" + I], xb)
        if i in CFG["twice"] and not turned:
            ts(64, out, out, 0.0, 255.0, ALU.max, ALU.min, xb, xb, xb)
        else:
            mm(64, out, T[back][:], T.vsb[:, 64 * i:64 * i + 64], True, True, [back, "v" + I], xb, xb)

    def products(i, final):
        k, q = i % 2, i // 2
        h, b = q // 2, q % 2
        tag[0] = "v%d" % i
        ps, bank = XB[CFG["xbank"][i]]
        for s in range(D):
            c = 768 * q + 128 * s
            tt(64, T.pv[:, c + 64 * k:c + 64 * k + 64], T.p[:, 384 * i + 64 * s:384 * i + 64 * s + 64], ps[:, 0:64], ALU.mult,
               ["p%d" % i, bank], ["pv%d_%d" % (i, s)], [bank])
            if k:
                out = PK[h][:, 48 * b + s:48 * b + 48:6] if final else PK[h][:, 6 * b + s:96:12]
                mm(256, out, T.pv[:, c:c + 128], T.b8[:, 0:8], True, True,
                   ["pv%d_%d" % (i - 1, s), "pv%d_%d" % (i, s), "b8"], ["k%d" % h], ["pk%d" % h])
        if final and k:
            tag[0] = "t%d" % h
            act(64, T.ks[:, 48 * q:48 * q + 48], PK[h][:, 48 * b:48 * b + 48], ["k%d" % h], ["ks%d" % q], ["pk%d" % h])
            send("k%d" % q, ["ks%d" % q])
            if rank // 4 == h:
                c = 48 * q + 12 * (rank % 4)
                act(64, T.kl[:, 96 * b + 12 * me:96 * b + 12 * me + 12], T.ks[:, c:c + 12], ["ks%d" % q], ["kl%d" % b])

    def sums(i, t, turned):
        q, k, I, a, h = i // 2, i % 2, str(i), 384 * i, i // 4
        tag[0] = "w" + I
        ps, bank = XB[CFG["xbank"][q]]
        wb, xb, out = ["pw%d" % k], [bank], ps[:, 0:128]
        wq = T.wq[0:112, 128 * (q % 2):128 * (q % 2) + 128]
        sel = lambda c: T.sel[0:112, 128 * c:128 * c + 128]
        fused = i in CFG["fused"]
        kept = T.wk[:, 384 * q:384 * q + 384]
        if t == 0 or not fused:
            for s in range(3):
                c = 7 * h + 3 * k + s
                mm(128, PW[k][:, 128 * s:128 * s + 128], sel(c), wq, True, True, ["wq", "sel%d" % c], wb, wb)
        tag[0] = "m" + I
        if fused and t > 0:
            op("v", lambda e: e.tensor_tensor(T.pw[:, a:a + 384], sources(i, t % 2), kept, ALU.mult), 0.05 + 384 * CFG["gc"] * cyc,
               winall(t % 2) + ["off%d" % h, "wk" + I], ["m" + I])
        else:
            tt(384, T.pw[:, a:a + 384], T.p[:, a:a + 384], PW[k][:, 0:384], ALU.mult, ["p" + I] + wb, ["m" + I], wb)
        if fused and t == 0:
            tag[0] = "k" + I
            act(384, kept, PW[k][:, 0:384], wb, ["wk" + I], wb)
            tag[0] = "m" + I
        c, there, back = (14, "turn", "unturn") if turned else (7 * h + 6, "idh", "idb")
        if k == 0:
            mm(128, out, sel(c), wq, True, False, ["wq", "sel%d" % c], xb, xb)
        for s in range(3):
            mm(128, out, T[there][:], T.pw[:, a + 128 * s:a + 128 * s + 128], False, k == 1 and s == 2, [there, "m" + I], xb, xb)
        if k == 1:
            tag[0] = "n%d" % q
            v, names = T.vsb[:, 128 * q:128 * q + 128], vall[2 * q:2 * q + 2]
            if q in CFG["aclamp"]:
                op("s", lambda e: e.activation(out, out, ACT.Relu, T.top[:], -1.0), 128 * cyc, xb + ["top"], xb, xb)
                op("s", lambda e: e.activation(v, out, ACT.Relu, T.top[:], -1.0), 128 * cyc, xb + ["top"], names, xb)
            else:
                ts(128, v, out, 0.0, 255.0, ALU.max, ALU.min, xb, names, xb)
            if q in CFG["twice"] and not turned:
                ts(128, out, out, 0.0, 255.0, ALU.max, ALU.min, xb, xb, xb)
            else:
                mm(128, out, T[back][:], v, True, True, [back] + names, xb, xb)

    def products(q, final):
        h, b = q // 2, q % 2
        tag[0] = "v%d" % q
        ps, bank = XB[CFG["xbank"][q]]
        for s in range(D):
            c = 768 * q + 128 * s
            tt(128, T.pv[:, c:c + 128], T.p[:, c:c + 128], ps[:, 0:128], ALU.mult, ["p%d" % (2 * q + s // 3), bank], ["pv%d_%d" % (q, s)], [bank])
            out = PK[h][:, 48 * b + s:48 * b + 48:6] if final else PK[h][:, 6 * b + s:96:12]
            mm(256, out, T.pv[:, c:c + 128], T.b8[:, 0:8], True, True, ["pv%d_%d" % (q, s), "b8"], ["k%d" % h], ["pk%d" % h])
        if final:
            tag[0] = "t%d" % h
            act(64, T.ks[:, 48 * q:48 * q + 48], PK[h][:, 48 * b:48 * b + 48], ["k%d" % h], ["ks%d" % q], ["pk%d" % h])
            send("k%d" % q, ["ks%d" % q])
            if rank // 4 == h:
                c = 48 * q + 12 * (rank % 4)
                act(64, T.kl[:, 96 * b + 12 * me:96 * b + 12 * me + 12], T.ks[:, c:c + 12], ["ks%d" % q], ["kl%d" % b])

    def spread_dma(t, groups, after, lag):
        u = (t + 1) % 2
        for j in groups:
            dma("y", "dw%d" % t, T.win[16 * j:16 * j + 16, W * u:W * u + 256 * nd], T.vsb[0:16 * nd, 0:256], vall[0:4] + after,
                [bydma(u)[j]] + [x for jj in range(nd // 2) for x in part(u, 0, jj)], lag=lag)

    def spread(h, t):
        u = (t + 1) % 2
        tag[0] = "e%d" % h
        first = nd // 2 if h == 0 else 0
        if first:
            spread_dma(t, range(CFG["early"]), [], CFG["td"][0])
        if h == 1 and CFG["fine"]:
            for b, (i, m) in enumerate(CFG["fine"]):
                tag[0] = "e%d" % (2 + b)
                n = 64 * m
                for k in range(2):
                    bank = ["pe%d" % k]
                    for j in range(4 * k, 4 * k + 4):
                        mm(n, PE[k][:, n * (j % 4):n * (j % 4) + n], block(T.rep, j), T.vsb[:, 64 * i:64 * i + n],
                           True, True, vall[i:i + m] + ["rep%d" % j], bank, bank)
                    for j in range(4 * k, 4 * k + 4):
                        c = W * u + 2048 + 256 * j + 64 * (i - 4)
                        act(n, T.win[:, c:c + n], PE[k][:, n * (j % 4):n * (j % 4) + n], bank,
                            ["win%d_1_%d_%d" % (u, j, x % 4) for x in range(i, i + m)], bank)
            return
        for jj in range(first, 4):
            bank = ["pe%d" % (jj % 2)]
            for j in (2 * jj, 2 * jj + 1):
                c = 4 + j if first else j
                mm(256, PE[jj % 2][:, 256 * (j % 2):256 * (j % 2) + 256], block(T.rep, c), T.vsb[:, 256 * h:256 * h + 256],
                   True, True, vall[4 * h:4 * h + 4] + ["rep%d" % c], bank, bank)
            c = W * u + 2048 * h + 512 * jj
            (cp if (h, jj) in CFG["vspread"] else act)(512, T.win[:, c:c + 512], PE[jj % 2][:], bank, part(u, h, jj), bank)

    def renew(h, sl, own):
        H = str(h)
        tag[0] = "t" + H
        a, z = 96 * h, 16 * h
        kb = ["pk" + H]
        c96 = lambda t: t[:, a:a + 96]
        c16 = lambda t: t[:, z:z + 16]
        back = lambda t, o: t[:, o + 95:o - 1 if o else None:-1]
        last = lambda t, o: t[:, o + 5:o + 96:6]
        ew, sx = PK[h][:, 96:192], PK[h][:, 192:288]
        if own:
            n = 2 * (rank // 4) + h
            K, kn, arr = c96(T.kl), "kl" + H, ("ark%d" % n, "k%d" % n, CFG["tk"])
            scb, so, bc, bo, src, pxn = PK[h], 0, PK[h], 320, T.po, "po" + H
        else:
            K, kn, arr = PK[h][:, 0:96], "k" + H, None
            scb, so, bc, bo, src, pxn = T.scb, a, T.bc, a, T.px, "px" + H
        keyn, px = "key%d" % sl, c96(src)
        scan(96, scb[:, so:so + 96], T.dmax[:], K, ALU.add, ALU.max, ["dmax", kn], ["scb" + H], kb, arr)
        cp(64, T.key[:, 16 * sl:16 * sl + 16], last(scb, so), ["scb" + H], [keyn], kb if own else [])
        if not own:
            send("c%d" % sl, [keyn])
        tag[0] = "r" + H
        scan(96, c96(T.scw), T.dmin[:], K, ALU.add, ALU.min, ["dmin", kn], ["scw" + H], kb, arr)
        if nd and not own and h == 0:
            spread_dma(sl // 2, range(CFG["early"], 8), ["scw0"], CFG["td"][1])
        tt(96, c96(T.nb), scb[:, so:so + 96], K, ALU.not_equal, ["scb" + H, kn], ["nb" + H], kb)
        scan(96, back(bc, bo), back(T.drev, 0), back(T.scw, a), ALU.add, ALU.min, ["drev", "scw" + H], ["bc" + H], kb if own else [])
        scan(96, c96(T.sb), c96(T.nb), sx, ALU.mult, ALU.max, ["nb" + H, "sx" + H], ["sb" + H], kb)
        tt(96, ew, bc[:, bo:bo + 96], K, ALU.is_equal, ["bc" + H, kn], ["ew" + H], kb)
        tt(96, c96(T.z), px, ew, ALU.mult, ["ew" + H, pxn], ["z" + H], kb)
        scan(64, c96(T.st), T.keeph[:], c96(T.z), ALU.mult, ALU.add, ["keeph", "z" + H], ["st" + H])
        if CFG["uuv"]:
            ut, uo, tw, ub = T.uu, z, T.uu[:, 32 + z:48 + z], []
            ts(64, T.uu[:, 64 + z:80 + z], last(T.st, a), 56.0, None, ALU.mult, None, ["st" + H], ["u1" + H])
            ts(64, tw, last(T.st, a), 2048.0, None, ALU.add, None, ["st" + H], ["tw" + H])
            tt(64, c16(T.uu), T.uu[:, 64 + z:80 + z], last(T.sb, a), ALU.add, ["u1" + H, "sb" + H], ["uu" + H])
        else:
            ut, uo, tw, ub = PK[h], 288, PK[h][:, 304:320], kb
            mm(256, ut[:, uo:uo + 16], T.idf[:], last(T.sb, a), True, False, ["idf", "sb" + H], ["uu" + H], kb)
            mm(64, ut[:, uo:uo + 16], T.i56[:], last(T.st, a), False, True, ["i56", "st" + H], ["uu" + H], kb)
            mm(64, tw, T.idh[:], T.coffh[:, 96:112], True, False, ["idh", "coffh"], ["tw" + H], kb)
            mm(64, tw, T.idh[:], last(T.st, a), False, True, ["idh", "st" + H], ["tw" + H], kb)
        tag[0] = "o" + H
        if own:
            tt(64, T.tot[:, z:z + 14], T.key[:, 16 * sl + 2:16 * sl + 16], ut[:, uo:uo + 14], ALU.add, ["uu" + H, keyn], ["tot" + H], ub)
            tt(64, T.tot[:, z + 14:z + 16], T.key[:, 16 * sl:16 * sl + 2], ut[:, uo + 14:uo + 16], ALU.add, ["uu" + H, keyn], ["totb" + H], ub)
        else:
            tt(64, c16(T.tot), T.cin[:, 16 * sl:16 * sl + 16], ut[:, uo:uo + 16], ALU.add, ["uu" + H], ["tot" + H, "totb" + H], ub,
               arr=("arc%d" % sl, "c%d" % sl, CFG["ring"]))
        ts(64, c16(T.nwv), c16(T.tot), 3, 4095, ALU.arith_shift_right, ALU.bitwise_and, ["tot" + H, "totb" + H], ["nwv" + H])
        tt(64, T.dpad[:, a:a + 96:6], c16(T.nwv), tw, ALU.subtract, ["nwv" + H, "tw" + H], ["dpad" + H], ub)
        scan(96, c96(T.db), T.keep[:], c96(T.dpad), ALU.mult, ALU.add, ["keep", "dpad" + H], ["db" + H])
        tt(96, ew, c96(T.db), ew, ALU.mult, ["ew" + H, "db" + H], ["ew" + H], kb)
        tt(96, px, px, ew, ALU.add, [pxn, "ew" + H], [pxn], kb)
        if own:
            for n in range(8):
                for jj in range(4):
                    place(lambda m: PK[h][32 * jj:32 * jj + m, 416 + n:512:8], n,
                          lambda lo: src[:, a + 12 * (2 * jj + lo):a + 12 * (2 * jj + lo) + 12], 12, [pxn], ["cv" + H], kb)
            for b in range(2):
                ts(64, T.yo[:, :, 16 * b + 8 * h:16 * b + 8 * h + 8], PK[h][:, 416 + 48 * b:464 + 48 * b], 2048.0, None, ALU.add, None,
                   ["cv" + H], ["yo%d" % (2 * h + b)], kb)
        else:
            lists(h, sl < 4)

    def give_back(h):
        dma("y", "dsy%d" % h, T.sy[4 * h:4 * h + 4], T.vsb[:, 256 * h:256 * h + 256], r=vall[4 * h:4 * h + 4], w=["sy%d" % h])
        if rank // 4 == h:
            c = 32 * (rank % 4)
            dma("y", "doy", T.ly[me], T.vsb[c:c + 32, 256 * h:256 * h + 256], r=vall[4 * h:4 * h + 4], w=["ly"])

    for t in range(RO):
        final = t == RO - 1
        now[:] = [t, "L" if final else ""]
        for i in range(8):
            gather(i, t % 2)
        if final:
            send("s", ["px0", "px1"])
            cp(64, T.sl[:, 2 * me:2 * me + 2, :], T.px[:, 24 * rank:24 * rank + 24], ["px0", "px1"], ["slo"])
        for q in range(6):
            if q >= 2:
                products(q - 2, final)
            if final and q == 3:
                send("y0", ["sy0"])
            if q < 4:
                sums(2 * q, t, nd and q < 2 and not final)
                sums(2 * q + 1, t, nd and q < 2 and not final)
            if final and q in (1, 3):
                give_back(q // 2)
        if not final:
            spread(0, t)
            spread(1, t)
            for h in range(2):
                renew(h, 2 * t + h, False)
    now[1] = "O"
    send("y1", ["sy1"])
    y = "y%d" % (rank // 4)
    for k in range(2):
        dma("y", "dya", T.ya[:, 256 * k:256 * k + 256], T.ly[:, 64 * k:64 * k + 64, :], r=["ly"], arr=("ar" + y, y, 5.0))
    for h in range(2):
        tag[0] = "x%d" % h
        cp(64, T.po[:, 96 * h:96 * h + 96], T.sl[:, :, 6 * h:6 * h + 6], ["slo"], ["po%d" % h], arr=("ars", "s", 6.5))
        keyed(h, T.po, "po")
        renew(h, 6 + h, True)
    dma("s", "dys", T.ys[:], T.yo[:], r=["yo0", "yo1", "yo2", "yo3"])
    return ops
